import numpy as np, ml_dtypes
CORES = [51,54,179,182]
N = 4
BF = ml_dtypes.bfloat16
def gentries(a):
    return np.ascontiguousarray(a.reshape(8, 16, -1).transpose(0, 2, 1)).reshape(8, -1)
def gtable(e):
    e = np.asarray(e); return np.ascontiguousarray(e.reshape(8, -1, 16).transpose(0, 2, 1)).reshape(128, -1).astype(np.int32)
V, A, VIS, ST = 1888, 256, 3, 3
def order(rng):
    return np.argsort(rng.random((N, 8, V)), axis=-1)
def by_order(o, ix):
    n = np.take_along_axis(o, ix.reshape(N, 8, V * 16), 2).reshape(N, 8, V, 16); b = np.empty_like(n)
    np.put_along_axis(b, o[..., None], n, 2)
    return b
def parts(rng):
    o = order(rng); i = np.arange(V)[None, None, :, None]; sh = (N, 8, V, 16)
    near = (i + rng.integers(-12, 13, sh)) % V; far = np.minimum((V * rng.random(sh) ** 2).astype(np.int64), V - 1)
    nm = by_order(o, np.where(rng.random(sh) < 0.5, near, far))
    return nm, rng.integers(0, 16, (N, 8, 16, V)), rng.integers(0, V, (N, 8, A)), rng.integers(0, 16, (N, 8, 16, A)), rng.integers(0, 32, (N, 8, 16, A))
def pack(nm, x, v, z, nz):
    return {"adj": np.stack([gtable(a.reshape(8, -1)) for a in nm]), "x": x.reshape(N, 128, V).astype(np.float32).astype(BF), "v0": np.stack([gtable(a) for a in v]),
            "z": z.reshape(N, 128, A).astype(np.float32).astype(BF), "nz": nz.reshape(N, 128, A).astype(np.float32).astype(BF)}
def setup_inputs(rng):
    return pack(*parts(rng))
def setup_inputs_loops(rng):
    nm, x, v, z, nz = parts(rng); o = order(rng); i = np.arange(V)[None, None, :]; m = ST + 1
    chain = np.where(i % m == m - 1, i - i % m + rng.integers(0, m, (N, 8, V)), (i + 1) % V)
    c = rng.integers(2, 3 * ST, (N, 8, 1)); base = i - i % c
    circle = np.minimum(base[..., None] + (rng.random((N, 8, V, 16)) * c[..., None]).astype(np.int64), V - 1)
    odd = (np.arange(8) % 2 == 1)[None, :, None, None]
    nm = by_order(o, np.where(odd, circle, chain[..., None]))
    alike = np.take_along_axis(x, np.take_along_axis(o, base, 2)[:, :, None, :], 3); y = np.empty_like(x)
    np.put_along_axis(y, o[:, :, None, :], alike, 3)
    return pack(nm, np.where(odd, y, x), v, z, nz)
def setup_inputs_crowd(rng):
    nm, x, v, z, nz = parts(rng); h = 12
    hub = 1 + np.argsort(rng.random((8, V - 2)), axis=-1)[:, :h]; hub[:, 0] = 0; hub[:, 1] = V - 1
    for g in range(6):
        for q in range(N):
            nm[q, g, hub[g]] = hub[g][rng.integers(0, h, (h, 16))]
        v[:, g] = hub[g][rng.integers(0, h, (N, A))]
    for q in range(N):
        p = rng.permutation(h); nm[q, 5, hub[5][p], 3] = hub[5][np.roll(p, -1)]
    x[:, 5] = x[:, 5, :, :1]; nz[:, 5] = 0; nz[:, 5, 3] = 31
    v[:, 6] = V - 1; v[:, 7] = 0
    return pack(nm, x, v, z, nz)
def setup_inputs_ties(rng):
    nm, x, v, z, nz = parts(rng)
    x[:, :2] = 7 + x[:, :2] % 2; z[:, :2] = 7 + z[:, :2] % 2; nz[:, :2] = nz[:, :2] % 2
    x[:, 2:4] = 15 * (x[:, 2:4] % 2); z[:, 2:4] = 15 * (z[:, 2:4] % 2); nz[:, 2:4] = 0
    v[:, 2, 0] = 0; nm[:, 2, 0] = V - 1; x[:, 2, :, V - 1] = 15; z[:, 2, :, 0] = 0
    x[:, 4] = 5; nz[:, 4] = 30 + nz[:, 4] % 2
    x[:, 5] = x[:1, 5]; nm[:, 5] = nm[:1, 5]; nz[:, 5] = 0
    nm[:, 6] = np.tile(nm[:, 6, :, :2], (1, 1, 8)); nz[:, 6] = nz[:, 6] % 4
    nz[:, 7] = 31
    return pack(nm, x, v, z, nz)
def setup_inputs_ends(rng):
    nm, x, v, z, nz = parts(rng)
    x[:, 0] = 15 - (x[:, 0] == 0).astype(np.int64); z[:, 0] = 0; nz[:, 0] = nz[:, 0] % 2
    x[:, 4] = (x[:, 4] == 0).astype(np.int64); z[:, 4] = 15; nz[:, 4] = nz[:, 4] % 4
    x[:, 1] = 7 + (x[:, 1] == 0).astype(np.int64); z[:, 1] = 7; nz[:, 1] = 24 + nz[:, 1] % 8
    level = ((int(rng.integers(0, N)) - np.arange(N)) % N)[:, None, None]
    x[:, 2] = 2 * level + x[:, 2] % 2; x[:, 3] = 2 * level; z[:, 2:4] = 0
    i = np.arange(V)[None, None, :, None]
    nm[:, 2:4] = by_order(order(rng), (i + 1 + rng.integers(0, 13, (N, 8, V, 16))) % V)[:, 2:4]
    v[:, 2:4] = np.argsort(rng.random((N, 2, V)), axis=-1)[..., :A]; v[:, 3, A - 1] = v[:, 3, 0]
    nz[:, 3] = nz[:, 3] % 31
    for q in range(N):
        k = int(rng.integers(0, 16)); nz[q, 3, k, 0] = 31; nz[q, 3, (k + 1 + int(rng.integers(0, 15))) % 16, A - 1] = 31
    return pack(nm, x, v, z, nz)
def setup_inputs_spread(rng):
    nm, x, v, z, nz = parts(rng); e = np.array([0.5, 1.0, 2.0, 4.0])
    ix = np.minimum(np.exp2(np.log2(V) * rng.random((N, 8, V, 16))).astype(np.int64) - 1, V - 1)
    nm = by_order(order(rng), ix); nm[:, 1::2] = V - 1 - ix[:, 1::2]
    x = np.minimum((16 * rng.random(x.shape) ** rng.choice(e, (N, 8, 1, V))).astype(np.int64), 15)
    z = np.minimum((16 * rng.random(z.shape) ** rng.choice(e, (N, 8, 1, A))).astype(np.int64), 15)
    nz = np.minimum((32 * rng.random(nz.shape) ** rng.choice(e, (N, 8, 16, 1))).astype(np.int64), 31)
    v = np.minimum((V * rng.random(v.shape) ** rng.choice(e, (N, 8, 1))).astype(np.int64), V - 1)
    return pack(nm, x, v, z, nz)
def check_inputs(d):
    bad = []
    for k, hi in (("adj", V - 1), ("v0", V - 1)):
        if np.min(d[k]) < 0 or np.max(d[k]) > hi: bad.append("range of " + k)
    for k, hi in (("x", 15), ("z", 15), ("nz", 31)):
        b = np.asarray(d[k]).astype(np.float32)
        if not np.all((b >= 0) & (b <= hi) & (b == np.floor(b))): bad.append("whole numbers of " + k)
    return bad
def reference(adj, x, v0, z, nz):
    nm = np.stack([gentries(b) for b in adj]).astype(np.int64).reshape(N, 8, V, 16)
    xt = np.ascontiguousarray(x.astype(np.float32).astype(np.int32).reshape(N, 8, 16, V).transpose(0, 1, 3, 2))
    w = np.ascontiguousarray(z.astype(np.float32).astype(np.int32).reshape(N, 8, 16, A).transpose(0, 1, 3, 2))
    no = np.ascontiguousarray(nz.astype(np.float32).astype(np.int64).reshape(N, 8, 16, A).transpose(0, 1, 3, 2))
    v = np.stack([gentries(b) for b in v0]).astype(np.int64)
    ph = np.full((N, 8, V, 16), 8, np.int64)
    r = np.arange(N)[:, None, None]; g = np.arange(8)[None, :, None]; pl = np.arange(ST)
    oldn = oldk = oldd = None
    for i in range(VIS):
        if i > 0: v = np.roll(v, 1, axis=0); w = np.roll(w, 1, axis=0)
        tn = np.full((N, 8, A, ST), -1, np.int64); tk = np.zeros((N, 8, A, ST), np.int64); ln = np.zeros((N, 8, A), np.int64)
        for s in range(ST):
            names = nm[r, g, v]
            far = np.sum(np.abs(xt[r[..., None], g[..., None], names] - w[:, :, :, None, :]), axis=4)
            k = np.argmax(ph[r, g, v] + np.roll(no, -(i * ST + s), axis=2) - far, axis=3)
            nv = np.take_along_axis(names, k[..., None], 3)[..., 0]
            here = pl == ln[..., None]
            tn = np.where(here, v[..., None], tn); tk = np.where(here, k[..., None], tk)
            hit = tn == nv[..., None]
            ln = np.where(np.any(hit, axis=3), np.argmax(hit, axis=3), ln + 1)
            tn = np.where(pl < ln[..., None], tn, -1); v = nv
        dd = np.sum(np.abs(xt[r, g, v] - w), axis=3)
        if i > 0:
            better = np.roll(dd < np.roll(oldd, 1, axis=0), -1, axis=0)
            for p in range(ST):
                q, h, b = np.nonzero(better & (oldn[..., p] >= 0))
                n = oldn[q, h, b, p]; kk = oldk[q, h, b, p]
                low = np.full((N, 8, V), A, np.int64); np.minimum.at(low, (q, h, n), b)
                m = low[q, h, n] == b; q, h, n, kk = q[m], h[m], n[m], kk[m]
                was = ph[q, h, n]; now = np.maximum(was - 3, 0); j = np.arange(len(q))
                now[j, kk] = np.minimum(was[j, kk] + 8, 20)
                ph[q, h, n] = now
        oldn, oldk, oldd = tn, tk, dd
    return {"yp": ph.transpose(0, 1, 3, 2).reshape(N, 128, V).astype(np.float32).astype(BF), "yv": np.stack([gtable(b) for b in v]).astype(np.float32)}

@@ -1,0 +1,553 @@
+from concourse.mybir import AluOpType as OP, ActivationFunctionType as AF
+
+V, A, VIS, ST = 1888, 256, 3, 3
+PW = V + 32
+OFF = 944
+MAG = 1.5 * 2.0 ** 34
+BIG = 4096.0
+H16, B16, F32, I32, U16 = "float16", "bfloat16", "float32", "int32", "uint16"
+
+NA = [48] * 6 + [40] * 6 + [24, 24] + [44] * 4
+NB = [60] * 6 + [56] * 6 + [88, 96] + [56] * 4
+VC, AC, CC = 32, 32, 64
+SHIFT, LATE = 1.0, 1.5
+TAIL = ("ph", "phk", "best", "widen", "turn", "chosen")
+PHASE = {"names": -0.26, "centred": 0.11, "open": 0.52, "ag0": 0.36, "ag1": 0.66, "ag2": 0.86, "sz0": -0.41, "sz1": 0.26, "sz2": 0.43,
+         "sg0": 0.33, "sg1": 0.42, "sg2": 0.79, "aa0": 0.67, "aa1": 0.78, "aa2": 1.25, "vc0": -0.09, "vc1": 0.65, "ca0": 0.55,
+         "va0": 0.06, "va1": 0.41, "relu": 0.78, "sumd": 0.53, "noise": 0.68, "ph": 1.08, "phk": 0.46, "sumr": 1.17,
+         "best": 1.08, "widen": 1.36, "turn": 1.37, "chosen": 1.61}
+PHI, GAT, SCA, CY, PE, ACT0 = 1.25, 1.56, 3.8, 0.833, 0.417, 80
+WAKE, SAME, LOOK, FAR = 140, 100, 60, 2400
+
+SB = {
+    "adjs": (V, I32), "xs": (V, B16), "z0": (A, B16), "z1": (A, B16), "z2": (A, B16),
+    "zr0": (16 * A, B16), "zr1": (16 * A, B16), "zr2": (16 * A, B16), "nzs": (A + 8, B16), "nzk": (A + 8, H16),
+    "v0s": (16, I32), "vl": (12 * 16, U16), "nm": (A, U16), "ee": (A, H16), "phg": (A, B16),
+    "dd": (16 * A, B16), "rr": (16 * A, B16), "ph": (PW, B16), "sc": (A, F32), "ll": (A, F32), "fd": (A, B16), "fa": (A, B16),
+    "do0": (A, B16), "do1": (A, B16), "di0": (A, B16), "di1": (A, B16), "fo1": (A, B16), "fo2": (A, B16), "fi1": (A, B16), "fi2": (A, B16),
+    "ia": (208, I32), "ib": (160, I32), "one": (256, B16), "idb": (128, B16), "idn": (128, B16), "idp": (128, B16),
+    "idm": (128, B16), "idq": (128, B16), "idh": (128, H16), "idk": (128, H16), "bo": (256, B16), "boh": (128, H16),
+    "gw": (16, B16), "g2": (16, F32), "mg": (16, B16), "msk": (128, F32), "mk2": (128, F32), "rst": (128, F32),
+    "bc": (8, U16), "lin": (48, U16), "dtab": (16, B16), "col": (8, F32), "spare": (48, F32),
+    "exa": (512, B16), "exb": (512, B16), "exh": (512, H16), "ut": (384, H16), "um": (768, H16), "cut": (512, B16),
+    "vf": (64, F32), "ki": (48, I32), "kb": (48, I32), "pp": (48, I32), "nn": (80, F32), "ex": (48, F32), "wk": (176, F32),
+    "un": (48, I32), "kr": (48, I32), "y0": (48, F32), "ku0": (48, U16), "ku1": (48, U16), "yy0": (48, F32), "yy1": (48, F32),
+    "ud0": (48, F32), "ud1": (48, F32), "ul0": (48, U16), "ul1": (48, U16), "uh0": (48, H16), "uh1": (48, H16),
+    "dl0": (768, B16), "dl1": (768, B16), "ab": (1536, B16), "pr": (1536, B16), "ok": (48, F32), "lst": (48, U16),
+    "tm": (A, B16), "tc": (A, B16), "yvs": (16, F32),
+}
+SCRATCH = {k: ("sbuf", [128, w], d) for k, (w, d) in SB.items()}
+SCRATCH.update({k: ("psum", [128, 512], F32) for k in ("kb0", "kb1", "sb0", "sb1", "sb2", "px0", "px1", "pz")})
+ARRIVALS = ["a_z1", "a_z2", "a_v10", "a_v11", "a_v20", "a_v21", "a_d0", "a_d1", "a_f10", "a_f11", "a_f20", "a_f21"]
+LOADS = ["l_adj", "l_x", "l_z", "l_v", "l_nz", "l_nw", "s_yv", "s_yp"]
+ENG = ("sV", "sA", "sP", "sG")
+SEMAPHORES = list(ENG) + ["sent"] + ARRIVALS + LOADS
+PLAN = []
+SPAN = [0]
+
+
+def r(name, a=0, b=None, step=1, parts=128):
+    if b is None:
+        b = SCRATCH[name][1][1]
+    return ("r", name, a, b, step, parts)
+
+
+def ind(win, off):
+    return ("i", win, off)
+
+
+def meet(x, y):
+    if x[1] >= y[2] or y[1] >= x[2]:
+        return False
+    if x[3] == 1 and y[3] == 1:
+        return True
+    return not set(range(x[1], x[2], x[3])).isdisjoint(range(y[1], y[2], y[3]))
+
+
+def links(ops):
+    hist, hard, soft, last = {}, [], [], {}
+    for i, (q, sem, inc, reads, writes, emit, cost, tag) in enumerate(ops):
+        hd, sf = set(), set()
+        acc = [(x, False) for x in reads] + [(x, True) for x in writes]
+        for x, wr in acc:
+            psum = SCRATCH[x[0]][0] == "psum"
+            for j, y, wr2 in hist.get(x[0], []):
+                if psum:
+                    (sf if ops[j][0] == q else hd).add(j)
+                elif (wr or wr2) and ops[j][1] is not None and meet(x, y):
+                    hd.add(j)
+        if sem not in ENG and q != "X":
+            if q in last:
+                sf.add(last[q])
+            last[q] = i
+        for x, wr in acc:
+            h = hist.setdefault(x[0], [])
+            if SCRATCH[x[0]][0] == "psum":
+                h[:] = [e for e in h if ops[e[0]][0] != q]
+            elif wr and x[3] == 1:
+                h[:] = [e for e in h if not (x[1] <= e[1][1] and e[1][2] <= x[2])]
+            h.append((i, x, wr))
+        hard.append(hd - {i})
+        soft.append(sf - {i})
+    for q in "VAP":
+        chain = sorted((o[7], i) for i, o in enumerate(ops) if o[0] == q and o[7] is not None)
+        for (_, a), (_, b) in zip(chain, chain[1:]):
+            soft[b].add(a)
+    return hard, soft
+
+
+def arrange(ops, hard, soft):
+    n = len(ops)
+    sender = {o[7]: i for i, o in enumerate(ops) if o[1] is None}
+    pre = []
+    for i, o in enumerate(ops):
+        p = [(j, ops[j][6][1] + (SAME if ops[j][0] == o[0] else WAKE)) for j in hard[i]] + [(j, ops[j][6][0]) for j in soft[i]]
+        if o[0] == "X":
+            p.append((sender[o[1]], FAR))
+        pre.append(p)
+    after = [[] for _ in ops]
+    for i, p in enumerate(pre):
+        for j, d in p:
+            after[j].append((i, d))
+    left = [len(p) for p in pre]
+    line = [i for i in range(n) if not left[i]]
+    for i in line:
+        for j, d in after[i]:
+            left[j] -= 1
+            if not left[j]:
+                line.append(j)
+    assert len(line) == n
+    rest = [0.0] * n
+    for i in reversed(line):
+        rest[i] = max([ops[i][6][1]] + [d + rest[j] for j, d in after[i]])
+    left = [len(p) for p in pre]
+    ready = [0.0] * n
+    free = {}
+    cand = [i for i in range(n) if not left[i]]
+    order = []
+    while cand:
+        t, q = min((max(ready[i], free.get(ops[i][0], 0.0)), ops[i][0]) for i in cand)
+        i = max((k for k in cand if ops[k][0] == q and ready[k] <= t + LOOK), key=lambda k: (rest[k], -k))
+        t = max(t, ready[i])
+        free[q] = t + ops[i][6][0]
+        cand.remove(i)
+        order.append(i)
+        for j, d in after[i]:
+            ready[j] = max(ready[j], t + d)
+            left[j] -= 1
+            if not left[j]:
+                cand.append(j)
+    SPAN[0] = max(free.values())
+    return order
+
+
+def plan_waits(ops, hard, order):
+    total, clock, done, out = {}, {}, {}, {}
+    for i in order:
+        q, sem, inc = ops[i][:3]
+        need = {}
+        for j in hard[i]:
+            s, c, k = done[j]
+            if need.get(s, (0, None))[0] < c:
+                need[s] = (c, k)
+        ck = clock.setdefault(q, {})
+        waits = []
+        for s, (c, k) in sorted(need.items(), key=lambda e: (-sum(e[1][1].values()), e[0])):
+            if ck.get(s, 0) < c:
+                waits.append((s, c))
+                for s2, c2 in k.items():
+                    if ck.get(s2, 0) < c2:
+                        ck[s2] = c2
+        if sem is not None:
+            total[sem] = total.get(sem, 0) + inc
+            k = dict(ck)
+            k[sem] = total[sem]
+            done[i] = (sem, total[sem], k)
+        out[i] = waits
+    return out, total
+
+
+def rank_program(g, core, T, topo):
+    rank = T.rank_of(core)
+    if rank is None:
+        return
+    n = len(T.cores)
+    nxt, prv, two = T.cores[(rank + 1) % n], T.cores[(rank - 1) % n], T.cores[(rank + 2) % n]
+    engines = topo.mask(core, nxt) & topo.mask(core, prv) & topo.mask(core, two)
+    width = bin(engines).count("1")
+    Q = {"V": g.vector, "A": g.scalar, "P": g.tensor, "G": g, "S": g.sync}
+    ops, posts, place = [], [], [None]
+
+    def ap(x):
+        if not isinstance(x, tuple):
+            return x
+        if x[0] == "i":
+            return ap(x[1]).indirect(ap(x[2]))
+        return T[x[1]][0:x[5], x[2]:x[3]:x[4]] if x[4] != 1 else T[x[1]][0:x[5], x[2]:x[3]]
+
+    def span(x):
+        return (x[1], x[2], x[3], x[4])
+
+    def at(j, kind, fn, *args):
+        late = SHIFT * (j // 6) + (LATE if j >= 14 or (j >= 12 and kind in TAIL) else 0)
+        place[0] = j + late + PHASE[kind]
+        res = fn(*args)
+        place[0] = None
+        return res
+
+    def count(x):
+        return 16 * count(x[2]) if x[0] == "i" else len(range(x[2], x[3], x[4]))
+
+    def price(q, out, ins, sem, per):
+        if sem:
+            return (50, per)
+        m = count(out)
+        wide = [x for x in [out] + ins if isinstance(x, tuple) and count(x) > 1]
+        if any(x[0] == "i" for x in wide):
+            d = 55 + m * CY * (SCA if out[0] == "i" else GAT)
+        elif q == "P":
+            d = 5 + max(min(64, count(ins[0])), m) * PE * PHI * (4 if SCRATCH[ins[0][1]][2] == F32 else 1)
+        elif q == "G":
+            d = (200 + 2 * m) * CY * 1.4
+        elif q == "A":
+            d = (ACT0 + m) * CY * PHI
+        else:
+            if per == 1.0 and all(SCRATCH[x[1]][2] in (B16, H16, U16) for x in wide):
+                per = 0.5
+            if per == 2.0 and any(SCRATCH[x[1]][0] == "psum" for x in wide):
+                per = 1.0
+            d = max(64, m * per) * CY * PHI
+        return (d, d)
+
+    def add(q, fn, out, ins, sem=None, inc=1, per=1.0):
+        reads, writes = [], []
+        for x in ins:
+            if isinstance(x, tuple):
+                reads += [span(x[1]), span(x[2])] if x[0] == "i" else [span(x)]
+        if isinstance(out, tuple):
+            if out[0] == "i":
+                writes.append(span(out[1]))
+                reads.append(span(out[2]))
+            else:
+                writes.append(span(out))
+        ops.append([q, sem or "s" + q, inc, reads, writes, fn, price(q, out, ins, sem, per), place[0]])
+
+    def copy(out, in_):
+        add("V", lambda: g.vector.tensor_copy(ap(out), ap(in_)), out, [in_])
+
+    def tt(out, a, b, op):
+        add("V", lambda: g.vector.tensor_tensor(ap(out), ap(a), ap(b), op), out, [a, b], per=2.0)
+
+    def ts(out, a, s1, op0, s2=None, op1=None):
+        if op1 is None:
+            add("V", lambda: g.vector.tensor_scalar(ap(out), ap(a), ap(s1), None, op0), out, [a, s1])
+        else:
+            add("V", lambda: g.vector.tensor_scalar(ap(out), ap(a), ap(s1), ap(s2), op0, op1), out, [a, s1, s2])
+
+    def fill(out, c):
+        add("V", lambda: g.vector.memset(ap(out), c), out, [])
+
+    def scan(out, d0, d1, init, op0, op1):
+        add("V", lambda: g.vector.tensor_tensor_scan(ap(out), ap(d0), ap(d1), init, op0, op1), out, [d0, d1])
+
+    def act(out, in_, func, scale=1.0):
+        add("A", lambda: g.scalar.activation(ap(out), ap(in_), func, scale=scale), out, [in_])
+
+    def mm(out, lhsT, rhs, start, stop):
+        add("P", lambda: g.tensor.matmul(ap(out), ap(lhsT), ap(rhs), start, stop), out, [lhsT, rhs])
+
+    def iota(out, pattern, base, cm):
+        add("G", lambda: g.iota(ap(out), pattern, base, cm), out, [])
+
+    def select(out, in_, pattern, op, c, base, cm):
+        add("G", lambda: g.affine_select(ap(out), ap(in_), pattern, op, c, base, cm), out, [in_])
+
+    def dma(out, in_, sem, when):
+        add("S", lambda: g.sync.dma_start(ap(out), ap(in_)), out, [in_], sem, 16, when)
+
+    def post(dst, out, in_, sem):
+        rid, pid = topo.addr(dst, core)
+        ops.append(["G", None, 0, [span(in_)], [],
+                    lambda: g.remote_dma(ap(out), ap(in_), T.sem[sem], T.sem.sent, pid, rid, engines), (300, 300), sem])
+        posts.append(sem)
+
+    def landed(buf, sem):
+        ops.append(["X", sem, width, [], [span(buf)], None, (0, 0), None])
+
+    def half(name, h, per=128):
+        return r(name, per * h, per * h + per)
+
+    zz, zr = ["z0", "z1", "z2"], ["zr0", "zr1", "zr2"]
+    for i in (1, 2):
+        landed(r(zz[i]), "a_z%d" % i)
+        landed(r("di%d" % (i - 1)), "a_d%d" % (i - 1))
+        for h in (0, 1):
+            landed(r("vl", 64 * i + 8 * h, 64 * i + 8 * h + 8), "a_v%d%d" % (i, h))
+            landed(half("fi%d" % i, h), "a_f%d%d" % (i, h))
+
+    dma(r("z0"), T.z[:], "l_z", 2600)
+    dma(r("v0s"), T.v0[:], "l_v", 3000)
+    dma(r("adjs"), T.adj[:], "l_adj", 6900)
+    dma(r("xs"), T.x[:], "l_x", 8800)
+    dma(r("nzs", 0, A), T.nz[:], "l_nz", 9200)
+    dma(r("nzs", A, A + 8), T.nz[:, 0:8], "l_nw", 9600)
+
+    fill(r("one"), 1.0)
+    iota(r("ia", 0, 128), [[1, 128]], 128, -1)
+    iota(r("ia", 128, 144), [[1, 16]], 1, 1)
+    iota(r("ia", 144, 152), [[16, 8]], 15, 0)
+    iota(r("ia", 152, 160), [[0, 8]], 0, 1)
+    iota(r("ia", 160, 208), [[1, 48]], 0, 0)
+    select(r("idb"), r("one", 0, 128), [[-1, 128]], OP.is_equal, 0.0, 0, 1)
+    select(r("bo", 128, 256), r("one", 0, 128), [[-16, 8], [0, 16]], OP.is_ge, 0.0, 0, 1)
+    select(r("bo", 0, 128), r("bo", 128, 256), [[16, 8], [0, 16]], OP.is_ge, 0.0, 15, -1)
+    group = r("bo", 0, 128, 16)
+    fill(r("ph"), 8.0)
+    fill(r("rst"), 0.0)
+    fill(r("rst", 0, 128, 16), -2.0 ** 26)
+    fill(r("mg", 0, 8), MAG)
+    fill(r("mg", 8, 16), -MAG)
+    post(nxt, r("z1"), r("z0"), "a_z1")
+    for k in range(16):
+        copy(r("zr0", k, 16 * A, 16), r("z0"))
+    ts(r("ib", 0, 144), r("ia", 0, 144), 15, OP.bitwise_and)
+    row = r("ib", 152, 153)
+    ts(row, r("ia", 152, 153), 15, OP.bitwise_and)
+    copy(r("bc"), r("ia", 144, 152))
+    copy(r("lin"), r("ia", 160, 208))
+    for name, c in (("idn", -1.0), ("idh", 1.0), ("idk", 2048.0), ("idp", 32768.0), ("idm", -BIG), ("idq", BIG)):
+        ts(r(name), r("idb"), c, OP.mult)
+    copy(r("boh"), r("bo", 0, 128))
+    ts(r("gw", 0, 8), group, -65536.0, OP.mult)
+    ts(r("gw", 8, 16), group, 32768.0, OP.mult)
+    copy(r("g2", 0, 8), group)
+    ts(r("g2", 8, 16), group, -1.0, OP.mult)
+    ts(r("msk"), r("ib", 0, 128), 0.0, OP.is_equal)
+    copy(r("mk2"), r("msk"))
+    fill(r("mk2", 31, 128, 32), 0.0)
+    ts(r("col", 0, 1), row, -1.0, OP.mult, 15.0, OP.add)
+    ts(r("col", 1, 2), row, float(V), OP.add)
+    ts(r("col", 2, 3), row, float(V + 16), OP.add)
+    ts(r("col", 3, 4), row, 15.0, OP.not_equal)
+    for t in (0, 1):
+        ts(r("spare", t, 48, 2), r("one", 0, 24), r("col", 1 + t, 2 + t), OP.mult)
+    copy(r("vl", 0, 16), r("v0s"))
+    ts(r("nzk"), r("nzs"), 16.0, OP.mult, r("col", 0, 1), OP.add)
+    ts(r("wk", 0, 16), r("ib", 128, 144), 0.0, OP.is_equal, 11.0, OP.mult)
+    ts(r("dtab"), r("wk", 0, 16), -3.0, OP.add)
+    fill(r("cut"), 0.0)
+    fill(r("cut", 31, 512, 32), 1.0)
+    for p in range(ST):
+        copy(r("ut", 128 * p, 128 * p + 128, 1, 32), r("msk", 0, 128, 1, 32))
+    fill(r("exa", 0, 512, 1, 32), 3 * BIG)
+    fill(r("one", 0, 256, 1, 32), -1.0)
+    for h in (0, 1):
+        a, b = r("exa", 256 * h, 256 * h + 256, 1, 32), r("exb", 256 * h, 256 * h + 256, 1, 32)
+        select(b, a, [[-16, 2], [0, 4], [1, 32]], OP.is_gt, BIG, 16, -1)
+        select(a, b, [[-16, 2], [0, 4], [1, 32]], OP.not_equal, 0.0, 16, -1)
+        select(r("exa", 256 * h, 256 * h + 256, 1, 16), r("one", 0, 256, 1, 16), [[1, 2], [2, 4], [0, 32]], OP.is_equal, 0.0, 8 * h, -1)
+    copy(r("exh", 0, 512, 1, 32), r("exa", 0, 512, 1, 32))
+    fill(r("exh", 31, 512, 32, 32), 0.0)
+
+    def spread(i):
+        for k in range(16):
+            select(r(zr[i], k, 16 * A, 16), r(zz[i]), [[0, A]], OP.is_ge, 0.0, 0, 0)
+
+    def ish(j):
+        return j // 6, (j % 6) // 2, 1 - j % 2
+
+    def nodes(slot, h):
+        return r("vl", 16 * slot + 8 * h, 16 * slot + 8 * h + 8)
+
+    def keys(h):
+        return r("kb%d" % h, 0, 128)
+
+    def cuts(a, b, most):
+        m = -(-(b - a) // most)
+        e = [a + 2 * (((b - a) // 2 * t) // max(m, 1)) for t in range(m + 1)]
+        return [(e[t], e[t + 1]) for t in range(m)]
+
+    bank = [0]
+
+    def half_step(j):
+        i, s, h = ish(j)
+        na, nb, late, kb = NA[j], NB[j], j in (12, 13), "kb%d" % h
+        wide = lambda name, a, b: r(name, 16 * (128 * h + a), 16 * (128 * h + b))
+        feats = lambda a, b: ind(r("xs"), r("nm", 128 * h + a, 128 * h + b))
+        at(j, "names", copy, half("nm", h), ind(r("adjs"), nodes(4 * i + s, h)))
+        at(j, "centred", ts, half("ee", h), half("nm", h), float(-OFF), OP.add)
+        at(j, "open", mm, keys(h), half("ee", h), r("idh"), True, False)
+        for t, (a, b) in enumerate(cuts(128 - nb, 128, AC)):
+            sb = r("sb%d" % (bank[0] % 3), 0, 16 * (b - a))
+            bank[0] += 1
+            at(j, "ag%d" % t, act, wide("dd", a, b), feats(a, b), AF.Copy)
+            at(j, "sz%d" % t, mm, sb, r("idn"), wide(zr[i], a, b), True, False)
+            at(j, "sg%d" % t, mm, sb, r("idb"), wide("dd", a, b), False, True)
+            at(j, "aa%d" % t, act, wide("rr", a, b), sb, AF.Abs, 0.5)
+        for t, (a, b) in enumerate(cuts(na, 128 - nb, VC)):
+            at(j, "vc%d" % t, tt, wide("dd", a, b), feats(a, b), wide(zr[i], a, b), OP.subtract)
+        for t, (a, b) in enumerate(cuts(na, 128 - nb, CC)):
+            at(j, "ca%d" % t, act, wide("rr", a, b), wide("dd", a, b), AF.Abs, 0.5)
+        for t, (a, b) in enumerate(cuts(0, na, VC)):
+            at(j, "va%d" % t, tt, wide("dd", a, b), feats(a, b), wide(zr[i], a, b), OP.subtract)
+        if na:
+            at(j, "relu", ts, wide("rr", 0, na), wide("dd", 0, na), 0.0, OP.max)
+            for k in range(16):
+                at(j, "sumd", mm, r(kb, k, 128, 16, na), r("dd", 2048 * h + k, 2048 * h + 16 * na, 16), r("gw", 8, 16), False, False)
+        a = 128 * h + 3 * i + s
+        at(j, "noise", mm, keys(h), r("nzk", a, a + 128), r("idk"), False, False)
+        if i == 2 and not late:
+            at(j, "ag0", act, half("phg", h), ind(r("ph"), nodes(4 * i + s, h)), AF.Copy)
+            at(j, "noise", mm, keys(h), half("phg", h), r("idp"), False, False)
+        for k in range(16):
+            at(j, "sumr", mm, r(kb, k, 128, 16), r("rr", 2048 * h + k, 2048 * h + 2048, 16), r("gw", 0, 8), False, k == 15 and not late)
+
+    def choice(j):
+        i, s, h = ish(j)
+        kb = "kb%d" % h
+        if j in (12, 13):
+            at(j, "ph", act, half("phg", h), ind(r("ph"), nodes(4 * i + s, h)), AF.Copy)
+            at(j, "phk", mm, keys(h), half("phg", h), r("idp"), False, True)
+        at(j, "best", scan, half("sc", h), r("rst"), keys(h), 0.0, OP.add, OP.max)
+        at(j, "widen", tt, half("ll", h), ind(half("sc", h), r("bc")), r("msk"), OP.mult)
+        right = r(kb, 152 + s, 176, 3)
+        at(j, "turn", mm, r(kb, 128 + s, 176, 3), half("ll", h), r("g2"), True, False)
+        at(j, "turn", mm, right, r("idb"), r("mg", 0, 8), False, False)
+        at(j, "turn", mm, right, r("idb"), r("mg", 8, 16), False, False)
+        at(j, "turn", mm, right, half("ll", h), r("g2", 0, 8), False, True)
+        at(j, "chosen", ts, nodes(4 * i + s + 1, h), right, float(OFF), OP.add)
+        if s == ST - 1:
+            if i < VIS - 1:
+                post(nxt, nodes(4 * i + 4, h), nodes(4 * i + 3, h), "a_v%d%d" % (i + 1, h))
+            distance(i, h)
+            if i < VIS - 1:
+                ts(half("ki", h, 24), r(kb, 128, 152), float(OFF), OP.add)
+
+    def distance(i, h):
+        far = r("kb%d" % h, 256, 384)
+        tt(half("fd", h), ind(r("xs"), nodes(4 * i + 3, h)), half(zz[i], h), OP.subtract)
+        act(half("fa", h), half("fd", h), AF.Abs)
+        mm(far, r("bo", 0, 128), half("fa", h), True, True)
+        if i > 0:
+            tt(half("fo%d" % i, h), far, half("di%d" % (i - 1), h), OP.is_lt)
+            post(prv, half("fi%d" % i, h), half("fo%d" % i, h), "a_f%d%d" % (i, h))
+        if i < VIS - 1:
+            act(half("do%d" % i, h), far, AF.Copy)
+
+    def trail(i):
+        w, nn, pp, ex = [lambda t, name=name: half(name, t, 16) for name in ("wk", "nn", "pp", "ex")]
+        yy, ud = r("yy%d" % i), r("ud%d" % i)
+        copy(r("vf"), r("vl", 64 * i, 64 * i + 64))
+        ts(r("kb"), r("ki"), 15 << 11, OP.bitwise_and)
+        tt(r("nn", 0, 48), r("vf", 0, 48), r("vf", 16, 64), OP.not_equal)
+        tt(r("nn", 48, 80), r("vf", 0, 32), r("vf", 32, 64), OP.not_equal)
+        tt(ex(0), r("vf", 0, 16), r("vf", 48, 64), OP.not_equal)
+        for s in range(ST):
+            tt(pp(s), r("kb", s, 48, 3), half("vf", s, 16), OP.add)
+        tt(w(2), nn(0), nn(3), OP.mult)
+        tt(w(3), nn(0), nn(1), OP.mult)
+        tt(w(7), nn(3), nn(4), OP.mult)
+        tt(r("wk", 0, 32), r("pp", 16, 48), r("pp", 0, 32), OP.subtract)
+        tt(w(9), nn(0), nn(2), OP.max)
+        tt(w(10), w(3), nn(2), OP.mult)
+        tt(w(8), w(7), ex(0), OP.mult)
+        tt(r("wk", 64, 96), r("wk", 32, 64), r("wk", 0, 32), OP.mult)
+        tt(w(6), nn(3), w(1), OP.mult)
+        tt(ex(1), w(8), w(9), OP.mult)
+        tt(pp(1), pp(2), w(5), OP.subtract)
+        tt(w(7), w(4), w(6), OP.add)
+        tt(ex(2), w(8), w(10), OP.mult)
+        tt(pp(0), pp(2), w(7), OP.subtract)
+        ts(r("un"), r("pp"), 2047, OP.bitwise_and)
+        ts(r("kr"), r("pp"), 11, OP.arith_shift_right)
+        tt(r("y0"), r("un"), r("spare"), OP.subtract)
+        copy(r("ku%d" % i), r("kr"))
+        tt(yy, r("y0"), r("ex"), OP.mult)
+        tt(ud, yy, r("spare"), OP.add)
+        copy(r("ul%d" % i), ud)
+        copy(r("uh%d" % i), ud)
+        act(r("dl%d" % i), ind(r("dtab"), r("ku%d" % i)), AF.Copy)
+
+    def region(p, h, a=0, b=256, step=1):
+        name, c = ("px%d" % h, 256 * p) if p < 2 else ("pz", 256 * h)
+        return r(name, c + a, c + b, step)
+
+    def differences(i):
+        for p in range(ST):
+            mm(r("pz", 128 * p, 128 * p + 128, 1, 16), half("uh%d" % i, p, 16), r("idh"), True, True)
+        copy(r("ut", 0, 384, 1, 16), r("pz", 0, 384, 1, 16))
+        for e in range(6):
+            tt(half("um", e), ind(r("ud%d" % i), half("lin", e, 8)), r("mk2"), OP.mult)
+        for p, h in ((0, 1), (1, 1), (0, 0), (1, 0), (2, 1), (2, 0)):
+            mm(region(p, h), r("ut", 128 * p, 128 * p + 128, 1, 32), r("exh", 256 * h, 256 * h + 256, 1, 32), p == 0 or (p, h) == (2, 1), False)
+            for t in (0, 1):
+                mm(region(p, h, 128 * t, 128 * t + 128), r("boh"), half("um", 2 * p + h), False, False)
+
+    def renewed(i, p):
+        tt(r("tm"), ind(r("ph"), half("ul%d" % i, p, 16)), half("dl%d" % i, p, 256), OP.add)
+        ts(r("tc"), r("tm"), 0.0, OP.max, 20.0, OP.min)
+
+    def reinforce(i):
+        fi, yy = "fi%d" % (i + 1), "yy%d" % i
+        for h in (1, 0):
+            ts(r("cut", 256 * h + 127, 256 * h + 255, 32), r(fi, 128 * h + 31, 128 * h + 128, 32), r("col", 3, 4), OP.max)
+        for pair in (((0, 1), (1, 1)), ((0, 0), (1, 0)), ((2, 1), (2, 0))):
+            for p, h in pair:
+                for t in (0, 1):
+                    mm(region(p, h, 128 * t, 128 * t + 128), r("idm"), half(fi, h), False, False)
+                    mm(region(p, h, 128 * t + 31, 128 * t + 128, 32), r("idq"), r(fi, 128 * h + 31, 128 * h + 128, 32), False,
+                       t == 1 and (p, h) == pair[1])
+            for p, h in pair:
+                e, c = 2 * p + h, 16 * p + 8 * h
+                act(half("ab", e, 256), region(p, h), AF.Abs)
+                scan(half("pr", e, 256), half("ab", e, 256), half("cut", h, 256), 1.0, OP.min, OP.max)
+                for t in (0, 1):
+                    tt(r("ok", c + t, c + 8, 2), r("pr", 256 * e + 128 * t + 30, 256 * e + 128 * t + 128, 32), r(yy, c + t, c + 8, 2), OP.mult)
+                    ts(r("lst", c + t, c + 8, 2), r("ok", c + t, c + 8, 2), r("col", 1 + t, 2 + t), OP.add)
+        for p in range(ST):
+            if p > 0:
+                renewed(i, p)
+            for j in range(7, -1, -1):
+                copy(ind(r("ph"), r("lst", 16 * p + 2 * j, 16 * p + 2 * j + 2)), r("tc", 32 * j, 32 * j + 32))
+
+    spread(1)
+    post(two, r("z2"), r("z0"), "a_z2")
+    for i in range(VIS):
+        for j in range(6 * i, 6 * i + 6):
+            half_step(j)
+            if j == 13:
+                reinforce(0)
+                differences(1)
+                renewed(1, 0)
+                choice(12)
+            if j != 12:
+                choice(j)
+        if i < VIS - 1:
+            post(nxt, r("di%d" % i), r("do%d" % i), "a_d%d" % i)
+            trail(i)
+        if i == 0:
+            spread(2)
+            differences(0)
+            renewed(0, 0)
+    copy(r("yvs"), r("vl", 176, 192))
+    dma(T.yv[:], r("yvs"), "s_yv", 2500)
+    reinforce(1)
+    dma(T.yp[:], r("ph", 0, V), "s_yp", 4000)
+
+    if not PLAN:
+        hard, soft = links(ops)
+        PLAN.extend([hard, arrange(ops, hard, soft)])
+    hard, order = PLAN
+    waits, total = plan_waits(ops, hard, order)
+    for o in order:
+        q, sem, inc, emit = ops[o][0], ops[o][1], ops[o][2], ops[o][5]
+        if emit is None:
+            continue
+        for s, c in waits[o]:
+            Q[q].wait_ge(T.sem[s], c)
+        ins = emit()
+        if sem is not None:
+            ins.then_inc(T.sem[sem], inc)
+    g.wait_ge(T.sem.sent, width * len(posts))
+    for s in ENG + ("s_yv", "s_yp"):
+        g.sync.wait_ge(T.sem[s], total[s])

@@ -1,67 +1,73 @@
+import numpy as np
 from concourse.mybir import AluOpType as OP, ActivationFunctionType as AF
 
 V, A, VIS, ST = 1888, 256, 3, 3
-PW = V + 32
+PW = V + 64
 OFF = 944
 MAG = 1.5 * 2.0 ** 34
 BIG = 4096.0
 H16, B16, F32, I32, U16 = "float16", "bfloat16", "float32", "int32", "uint16"
 
-NA = [48] * 6 + [40] * 6 + [24, 24] + [44] * 4
-NB = [60] * 6 + [56] * 6 + [88, 96] + [56] * 4
-VC, AC, CC = 32, 32, 64
-SHIFT, LATE = 1.0, 1.5
-TAIL = ("ph", "phk", "best", "widen", "turn", "chosen")
-PHASE = {"names": -0.26, "centred": 0.11, "open": 0.52, "ag0": 0.36, "ag1": 0.66, "ag2": 0.86, "sz0": -0.41, "sz1": 0.26, "sz2": 0.43,
-         "sg0": 0.33, "sg1": 0.42, "sg2": 0.79, "aa0": 0.67, "aa1": 0.78, "aa2": 1.25, "vc0": -0.09, "vc1": 0.65, "ca0": 0.55,
-         "va0": 0.06, "va1": 0.41, "relu": 0.78, "sumd": 0.53, "noise": 0.68, "ph": 1.08, "phk": 0.46, "sumr": 1.17,
-         "best": 1.08, "widen": 1.36, "turn": 1.37, "chosen": 1.61}
-PHI, GAT, SCA, CY, PE, ACT0 = 1.25, 1.56, 3.8, 0.833, 0.417, 80
-WAKE, SAME, LOOK, FAR = 140, 100, 60, 2400
+KIND = "abbbbz" "accccz" "degffz"
+AC = 32
+STEP = {"late": 0.25, "shift": 0.25, "early": 1, "look": 30, "slack": 50, "turn01": 1, "turn00": 1, "turn11": 1, "turn10": 1, "flag": 0.05,
+        "far": 0.05, "runs": 0}
+TAIL = ("ph", "close", "best", "widen", "turn", "chosen")
+FLAG = ("end", "endabs", "far", "flag")
+SOLO = {"v2": "v1", "abs": "a1"}
+RUNS = [[range(18)],
+        [range(0, 6), range(6, 12), [12], [13], range(14, 18)],
+        [[0], range(1, 6), [6], range(7, 12), [12], [13], [14], range(15, 18)],
+        [range(0, 6), range(6, 12), range(12, 18)],
+        [range(0, 12), [12], [13], range(14, 18)]]
+ORDER, CUT, NUM = ({'V': [('v2', 0), ('v0', 0), ('centred', 0), ('best', -1), ('relu0', 0), ('widen', -1), ('v1', 0), ('end', -1), ('endabs', -1), ('names', 1), ('relu1', 0), ('flag', -1)], 'A': [('a0', -1), ('chosen', -2), ('a1', -1), ('ph0', 0), ('ph', 0), ('g0', 0), ('a2', -1), ('g2', 0), ('g1', 0), ('abs', 0)], 'P': [('sumd', -1), ('name', -1), ('far', -2), ('sum', -1), ('z1', 0), ('z2', 0), ('x0', 0), ('x1', 0), ('x2', 0), ('turn', -1), ('open', 0), ('z0', 1), ('close', 0)]}, {'a': (16, 50, 14, 30), 'g': (26, 46, 0, 34), 'b': (18, 36, 18, 28), 'c': (20, 38, 14, 46), 'd': (38, 20, 0, 56), 'e': (22, 6, 12, 34), 'f': (16, 40, 20, 40), 'z': (28, 20, 16, 32)}, {'late': 3.0, 'shift': 0.75, 'early': 1, 'look': 30, 'slack': 350, 'turn01': 7, 'turn00': 11, 'turn11': 13, 'turn10': 17, 'flag': 0.15, 'far': 0.3, 'runs': 4})
+PHI, GAT, SCA, CY, PE, ACT0 = 1.25, 1.56, 3.8, 0.833, 0.417, 64
+WAKE, SAME, FAR, FIRST = 140, 140, 2400, 3000
 
 SB = {
     "adjs": (V, I32), "xs": (V, B16), "z0": (A, B16), "z1": (A, B16), "z2": (A, B16),
     "zr0": (16 * A, B16), "zr1": (16 * A, B16), "zr2": (16 * A, B16), "nzs": (A + 8, B16), "nzk": (A + 8, H16),
     "v0s": (16, I32), "vl": (12 * 16, U16), "nm": (A, U16), "ee": (A, H16), "phg": (A, B16),
-    "dd": (16 * A, B16), "rr": (16 * A, B16), "ph": (PW, B16), "sc": (A, F32), "ll": (A, F32), "fd": (A, B16), "fa": (A, B16),
+    "dd": (16 * A, B16), "rr": (16 * A, B16), "ph": (PW, B16), "num": (PW, F32), "sc": (A, F32), "ll": (A, F32), "fd": (A, B16), "fa": (A, B16),
     "do0": (A, B16), "do1": (A, B16), "di0": (A, B16), "di1": (A, B16), "fo1": (A, B16), "fo2": (A, B16), "fi1": (A, B16), "fi2": (A, B16),
-    "ia": (208, I32), "ib": (160, I32), "one": (256, B16), "idb": (128, B16), "idn": (128, B16), "idp": (128, B16),
-    "idm": (128, B16), "idq": (128, B16), "idh": (128, H16), "idk": (128, H16), "bo": (256, B16), "boh": (128, H16),
-    "gw": (16, B16), "g2": (16, F32), "mg": (16, B16), "msk": (128, F32), "mk2": (128, F32), "rst": (128, F32),
-    "bc": (8, U16), "lin": (48, U16), "dtab": (16, B16), "col": (8, F32), "spare": (48, F32),
-    "exa": (512, B16), "exb": (512, B16), "exh": (512, H16), "ut": (384, H16), "um": (768, H16), "cut": (512, B16),
+    "ia": (176, I32), "ib": (144, I32), "one": (128, B16), "idb": (128, B16), "idn": (128, B16), "idp": (128, B16),
+    "idm": (128, B16), "idh": (128, H16), "idk": (128, H16), "bo": (256, B16), "bw": (256, B16),
+    "gw": (16, B16), "g2": (16, F32), "mg": (16, B16), "msk": (128, F32), "rst": (128, F32), "rs2": (768, B16),
+    "bc": (8, U16), "dtab": (32, B16), "col": (4, F32), "spare": (24, F32), "lf": (48, F32),
+    "exa": (768, B16), "exb": (768, B16), "exc": (512, B16), "exh": (768, H16), "ut": (768, H16), "um": (768, H16), "yy0": (48, F32), "yy1": (48, F32),
     "vf": (64, F32), "ki": (48, I32), "kb": (48, I32), "pp": (48, I32), "nn": (80, F32), "ex": (48, F32), "wk": (176, F32),
-    "un": (48, I32), "kr": (48, I32), "y0": (48, F32), "ku0": (48, U16), "ku1": (48, U16), "yy0": (48, F32), "yy1": (48, F32),
-    "ud0": (48, F32), "ud1": (48, F32), "ul0": (48, U16), "ul1": (48, U16), "uh0": (48, H16), "uh1": (48, H16),
-    "dl0": (768, B16), "dl1": (768, B16), "ab": (1536, B16), "pr": (1536, B16), "ok": (48, F32), "lst": (48, U16),
+    "un": (48, I32), "kr": (48, I32), "y0": (48, F32), "ku": (48, U16), "uh": (48, H16), "ul0": (48, U16), "ul1": (48, U16),
+    "dl0": (768, B16), "dl1": (768, B16), "ab": (2560, B16), "pr": (2560, B16), "ok": (48, F32), "lst": (48, U16),
     "tm": (A, B16), "tc": (A, B16), "yvs": (16, F32),
 }
 SCRATCH = {k: ("sbuf", [128, w], d) for k, (w, d) in SB.items()}
-SCRATCH.update({k: ("psum", [128, 512], F32) for k in ("kb0", "kb1", "sb0", "sb1", "sb2", "px0", "px1", "pz")})
+SCRATCH.update({k: ("psum", [128, 512], F32) for k in ("kb0", "kb1", "sb0", "sb1", "sb2", "px0", "px1", "px2")})
 ARRIVALS = ["a_z1", "a_z2", "a_v10", "a_v11", "a_v20", "a_v21", "a_d0", "a_d1", "a_f10", "a_f11", "a_f20", "a_f21"]
 LOADS = ["l_adj", "l_x", "l_z", "l_v", "l_nz", "l_nw", "s_yv", "s_yp"]
 ENG = ("sV", "sA", "sP", "sG")
 SEMAPHORES = list(ENG) + ["sent"] + ARRIVALS + LOADS
 PLAN = []
 SPAN = [0]
+SEEN = {}
+
+
+def view(name, parts, *ix):
+    key = (name, tuple((s.start, s.stop, s.step) for s in ix))
+    if key not in SEEN:
+        shape = SCRATCH[name][1][1:]
+        el = np.arange(int(np.prod(shape))).reshape(shape)[ix].reshape(-1)
+        SEEN[key] = (sum(1 << int(e) for e in el), len(el))
+    return ("r", name, (slice(*parts) if isinstance(parts, tuple) else slice(0, parts),) + ix) + SEEN[key]
 
 
 def r(name, a=0, b=None, step=1, parts=128):
-    if b is None:
-        b = SCRATCH[name][1][1]
-    return ("r", name, a, b, step, parts)
+    if len(SCRATCH[name][1]) == 3:
+        return view(name, parts, slice(None), slice(None))
+    return view(name, parts, slice(a, SCRATCH[name][1][1] if b is None else b, None if step == 1 else step))
 
 
 def ind(win, off):
     return ("i", win, off)
-
-
-def meet(x, y):
-    if x[1] >= y[2] or y[1] >= x[2]:
-        return False
-    if x[3] == 1 and y[3] == 1:
-        return True
-    return not set(range(x[1], x[2], x[3])).isdisjoint(range(y[1], y[2], y[3]))
 
 
 def links(ops):
@@ -70,29 +76,30 @@ def links(ops):
         hd, sf = set(), set()
         acc = [(x, False) for x in reads] + [(x, True) for x in writes]
         for x, wr in acc:
-            psum = SCRATCH[x[0]][0] == "psum"
-            for j, y, wr2 in hist.get(x[0], []):
+            psum = SCRATCH[x[1]][0] == "psum"
+            for j, y, wr2 in hist.get(x[1], []):
                 if psum:
                     (sf if ops[j][0] == q else hd).add(j)
-                elif (wr or wr2) and ops[j][1] is not None and meet(x, y):
+                elif (wr or wr2) and ops[j][1] is not None and x[3] & y[3]:
                     hd.add(j)
-        if sem not in ENG and q != "X":
+        if q in "GS":
             if q in last:
                 sf.add(last[q])
             last[q] = i
         for x, wr in acc:
-            h = hist.setdefault(x[0], [])
-            if SCRATCH[x[0]][0] == "psum":
+            h = hist.setdefault(x[1], [])
+            if SCRATCH[x[1]][0] == "psum":
                 h[:] = [e for e in h if ops[e[0]][0] != q]
-            elif wr and x[3] == 1:
-                h[:] = [e for e in h if not (x[1] <= e[1][1] and e[1][2] <= x[2])]
+            elif wr and x[2][0].stop == 128:
+                h[:] = [e for e in h if e[1][3] & ~x[3]]
             h.append((i, x, wr))
         hard.append(hd - {i})
         soft.append(sf - {i})
-    for q in "VAP":
-        chain = sorted((o[7], i) for i, o in enumerate(ops) if o[0] == q and o[7] is not None)
-        for (_, a), (_, b) in zip(chain, chain[1:]):
-            soft[b].add(a)
+    for q in ORDER:
+        for run in RUNS[NUM["runs"]]:
+            chain = sorted((o[7], i) for i, o in enumerate(ops) if o[0] == q and o[7] is not None and o[7][1] in run)
+            for (_, a), (_, b) in zip(chain, chain[1:]):
+                soft[b].add(a)
     return hard, soft
 
 
@@ -127,7 +134,18 @@ def arrange(ops, hard, soft):
     order = []
     while cand:
         t, q = min((max(ready[i], free.get(ops[i][0], 0.0)), ops[i][0]) for i in cand)
-        i = max((k for k in cand if ops[k][0] == q and ready[k] <= t + LOOK), key=lambda k: (rest[k], -k))
+        mine = sorted((k for k in cand if ops[k][0] == q), key=lambda k: (-rest[k], k))
+        i = None
+        for m, k in enumerate(mine):
+            if ready[k] <= t + NUM["look"] and all(t + ops[k][6][0] <= ready[u] + NUM["slack"] for u in mine[:m] if rest[u] > rest[k] + 300):
+                i = k
+                break
+        if i is None:
+            i = min(mine, key=lambda k: (max(ready[k], t) - rest[k], k))
+            other = [max(ready[k], free.get(ops[k][0], 0.0)) for k in cand if ops[k][0] != q]
+            if other and min(other) < ready[i]:
+                free[q] = min(other) + 1.0
+                continue
         t = max(t, ready[i])
         free[q] = t + ops[i][6][0]
         cand.remove(i)
@@ -176,27 +194,29 @@ def rank_program(g, core, T, topo):
     engines = topo.mask(core, nxt) & topo.mask(core, prv) & topo.mask(core, two)
     width = bin(engines).count("1")
     Q = {"V": g.vector, "A": g.scalar, "P": g.tensor, "G": g, "S": g.sync}
-    ops, posts, place = [], [], [None]
+    ops, posts, place, adding = [], [], [None], {}
+
+    def at(j, kind, fn, *args):
+        slot = j + NUM["shift"] * (j // 6) + (NUM["late"] if j >= 14 or (j >= 12 and kind in TAIL) else 0)
+        if j == 1 and kind == "names":
+            slot = 0.01
+        like = SOLO.get(kind, kind) if KIND[j] in "ag" else kind
+        place[0] = [slot - d + m / len(o) for o in ORDER.values() for m, (k, d) in enumerate(o) if k == like][0] + 0.001 * (like != kind)
+        if j == 11 and kind in FLAG:
+            place[0] = 12 + 2 * NUM["shift"] + NUM["far" if kind == "far" else "flag"] + 0.001 * FLAG.index(kind)
+        place[0] = (place[0], j)
+        fn(*args)
+        place[0] = None
 
     def ap(x):
         if not isinstance(x, tuple):
             return x
         if x[0] == "i":
             return ap(x[1]).indirect(ap(x[2]))
-        return T[x[1]][0:x[5], x[2]:x[3]:x[4]] if x[4] != 1 else T[x[1]][0:x[5], x[2]:x[3]]
-
-    def span(x):
-        return (x[1], x[2], x[3], x[4])
-
-    def at(j, kind, fn, *args):
-        late = SHIFT * (j // 6) + (LATE if j >= 14 or (j >= 12 and kind in TAIL) else 0)
-        place[0] = j + late + PHASE[kind]
-        res = fn(*args)
-        place[0] = None
-        return res
+        return T[x[1]][x[2]]
 
     def count(x):
-        return 16 * count(x[2]) if x[0] == "i" else len(range(x[2], x[3], x[4]))
+        return 16 * x[2][4] if x[0] == "i" else x[4]
 
     def price(q, out, ins, sem, per):
         if sem:
@@ -204,11 +224,11 @@ def rank_program(g, core, T, topo):
         m = count(out)
         wide = [x for x in [out] + ins if isinstance(x, tuple) and count(x) > 1]
         if any(x[0] == "i" for x in wide):
-            d = 55 + m * CY * (SCA if out[0] == "i" else GAT)
+            d = (50 if q == "V" else 65) + m * CY * (SCA if out[0] == "i" else GAT)
         elif q == "P":
             d = 5 + max(min(64, count(ins[0])), m) * PE * PHI * (4 if SCRATCH[ins[0][1]][2] == F32 else 1)
         elif q == "G":
-            d = (200 + 2 * m) * CY * 1.4
+            d = (170 + 2 * m * CY) * PHI
         elif q == "A":
             d = (ACT0 + m) * CY * PHI
         else:
@@ -223,14 +243,16 @@ def rank_program(g, core, T, topo):
         reads, writes = [], []
         for x in ins:
             if isinstance(x, tuple):
-                reads += [span(x[1]), span(x[2])] if x[0] == "i" else [span(x)]
+                reads += [x[1], x[2]] if x[0] == "i" else [x]
         if isinstance(out, tuple):
             if out[0] == "i":
-                writes.append(span(out[1]))
-                reads.append(span(out[2]))
+                writes.append(out[1])
+                reads.append(out[2])
             else:
-                writes.append(span(out))
+                writes.append(out)
         ops.append([q, sem or "s" + q, inc, reads, writes, fn, price(q, out, ins, sem, per), place[0]])
+        for x in reads:
+            adding.pop(x[1], None)
 
     def copy(out, in_):
         add("V", lambda: g.vector.tensor_copy(ap(out), ap(in_)), out, [in_])
@@ -250,11 +272,15 @@ def rank_program(g, core, T, topo):
     def scan(out, d0, d1, init, op0, op1):
         add("V", lambda: g.vector.tensor_tensor_scan(ap(out), ap(d0), ap(d1), init, op0, op1), out, [d0, d1])
 
-    def act(out, in_, func, scale=1.0):
-        add("A", lambda: g.scalar.activation(ap(out), ap(in_), func, scale=scale), out, [in_])
+    def act(out, in_, func, scale=1.0, bias=0.0):
+        add("A", lambda: g.scalar.activation(ap(out), ap(in_), func, bias=ap(bias), scale=ap(scale)), out, [in_, scale, bias])
 
-    def mm(out, lhsT, rhs, start, stop):
-        add("P", lambda: g.tensor.matmul(ap(out), ap(lhsT), ap(rhs), start, stop), out, [lhsT, rhs])
+    def mm(out, lhsT, rhs, start):
+        ends = [True]
+        add("P", lambda: g.tensor.matmul(ap(out), ap(lhsT), ap(rhs), start, ends[0]), out, [lhsT, rhs])
+        if not start and adding.get(out[1]):
+            adding[out[1]][0] = False
+        adding[out[1]] = ends
 
     def iota(out, pattern, base, cm):
         add("G", lambda: g.iota(ap(out), pattern, base, cm), out, [])
@@ -267,100 +293,113 @@ def rank_program(g, core, T, topo):
 
     def post(dst, out, in_, sem):
         rid, pid = topo.addr(dst, core)
-        ops.append(["G", None, 0, [span(in_)], [],
-                    lambda: g.remote_dma(ap(out), ap(in_), T.sem[sem], T.sem.sent, pid, rid, engines), (300, 300), sem])
+        ops.append(["G", None, 0, [in_], [],
+                    lambda: g.remote_dma(ap(out), ap(in_), T.sem[sem], T.sem.sent, pid, rid, engines),
+                    (300, 300) if posts else (FIRST, FIRST), sem])
         posts.append(sem)
 
     def landed(buf, sem):
-        ops.append(["X", sem, width, [], [span(buf)], None, (0, 0), None])
+        ops.append(["X", sem, width, [], [buf], None, (0, 0), None])
 
     def half(name, h, per=128):
         return r(name, per * h, per * h + per)
+
+    def col(c):
+        return r("col", c, c + 1)
 
     zz, zr = ["z0", "z1", "z2"], ["zr0", "zr1", "zr2"]
     for i in (1, 2):
         landed(r(zz[i]), "a_z%d" % i)
         landed(r("di%d" % (i - 1)), "a_d%d" % (i - 1))
         for h in (0, 1):
-            landed(r("vl", 64 * i + 8 * h, 64 * i + 8 * h + 8), "a_v%d%d" % (i, h))
+            landed(half("vl", 8 * i + 4 * h, 8), "a_v%d%d" % (i, h))
             landed(half("fi%d" % i, h), "a_f%d%d" % (i, h))
 
-    dma(r("z0"), T.z[:], "l_z", 2600)
-    dma(r("v0s"), T.v0[:], "l_v", 3000)
-    dma(r("adjs"), T.adj[:], "l_adj", 6900)
-    dma(r("xs"), T.x[:], "l_x", 8800)
-    dma(r("nzs", 0, A), T.nz[:], "l_nz", 9200)
-    dma(r("nzs", A, A + 8), T.nz[:, 0:8], "l_nw", 9600)
+    dma(r("z0"), T.z[:], "l_z", 2300)
+    dma(r("v0s"), T.v0[:], "l_v", 2300)
+    dma(r("adjs"), T.adj[:], "l_adj", 6100)
+    dma(r("xs"), T.x[:], "l_x", 8000)
+    dma(r("nzs", 0, A), T.nz[:], "l_nz", 8200)
+    dma(r("nzs", A, A + 8), T.nz[:, 0:8], "l_nw", 8200)
 
+    place[0] = (-9.0, 0)
     fill(r("one"), 1.0)
-    iota(r("ia", 0, 128), [[1, 128]], 128, -1)
-    iota(r("ia", 128, 144), [[1, 16]], 1, 1)
-    iota(r("ia", 144, 152), [[16, 8]], 15, 0)
-    iota(r("ia", 152, 160), [[0, 8]], 0, 1)
-    iota(r("ia", 160, 208), [[1, 48]], 0, 0)
-    select(r("idb"), r("one", 0, 128), [[-1, 128]], OP.is_equal, 0.0, 0, 1)
-    select(r("bo", 128, 256), r("one", 0, 128), [[-16, 8], [0, 16]], OP.is_ge, 0.0, 0, 1)
-    select(r("bo", 0, 128), r("bo", 128, 256), [[16, 8], [0, 16]], OP.is_ge, 0.0, 15, -1)
-    group = r("bo", 0, 128, 16)
+    fill(r("exa", 0, 768, 1, 32), 3 * BIG)
+    fill(r("exc", 0, 512, 1, 32), -1.0)
     fill(r("ph"), 8.0)
     fill(r("rst"), 0.0)
+    fill(r("rs2"), 0.0)
+    for c, x in enumerate((MAG, -MAG)):
+        fill(half("mg", c, 8), x)
     fill(r("rst", 0, 128, 16), -2.0 ** 26)
-    fill(r("mg", 0, 8), MAG)
-    fill(r("mg", 8, 16), -MAG)
+    fill(r("rs2", 0, 256, 32), 2.0 ** 30)
+    fill(r("rs2", 256, 768, 64), 2.0 ** 30)
+    scan(r("num"), r("ph"), r("ph"), -16.0, OP.add, OP.add)
+    iota(r("ia", 128, 144), [[1, 16]], 1, 1)
+    iota(r("ia", 0, 128), [[1, 128]], 128, -1)
+    iota(r("ia", 144, 152), [[16, 8]], 15, 0)
+    iota(r("ia", 152, 160), [[0, 4], [16, 2]], V, 0)
+    iota(r("ia", 160, 176), [[0, 4], [16, 4]], V, 0)
+    select(r("idb"), r("one", 0, 128), [[-1, 128]], OP.is_equal, 0.0, 0, 1)
+    select(r("bo", 128, 256), r("one", 0, 128), [[-16, 8], [0, 16]], OP.is_ge, 0.0, 0, 1)
+    a, b = r("exa", 0, 256, 1, 32), r("exb", 0, 256, 1, 32)
+    select(b, a, [[-16, 2], [0, 4], [1, 32]], OP.is_gt, BIG, 16, -1)
+    select(r("bo", 0, 128), r("bo", 128, 256), [[16, 8], [0, 16]], OP.is_ge, 0.0, 15, -1)
     post(nxt, r("z1"), r("z0"), "a_z1")
+    post(two, r("z2"), r("z0"), "a_z2")
+    select(a, b, [[-16, 2], [0, 4], [1, 32]], OP.not_equal, 0.0, 16, -1)
+    select(r("exa", 0, 256, 1, 16), r("exc", 0, 256, 1, 16), [[1, 2], [2, 4], [0, 32]], OP.is_equal, 0.0, 0, -1)
+    group = r("bo", 0, 128, 16)
+    ts(r("ib"), r("ia", 0, 144), 15, OP.bitwise_and)
+    for h in (1, 0):
+        copy(half("vl", 4 * h, 8), half("v0s", h, 8))
+    row = col(0)
+    copy(row, r("ib", 143, 144))
+    ts(col(2), r("ib", 143, 144), -1.0, OP.mult, 15.0, OP.add)
+    ts(r("spare"), r("ia", 152, 176), row, OP.add)
+    ts(r("msk"), r("ib", 0, 128), 0.0, OP.is_equal)
+    ts(r("wk", 0, 16), r("ib", 128, 144), 0.0, OP.is_equal, 11.0, OP.mult)
     for k in range(16):
-        copy(r("zr0", k, 16 * A, 16), r("z0"))
-    ts(r("ib", 0, 144), r("ia", 0, 144), 15, OP.bitwise_and)
-    row = r("ib", 152, 153)
-    ts(row, r("ia", 152, 153), 15, OP.bitwise_and)
+        if k % 2:
+            copy(r("zr0", k, 16 * A, 16), r("z0"))
+        else:
+            act(r("zr0", k, 16 * A, 16), r("z0"), AF.Copy)
     copy(r("bc"), r("ia", 144, 152))
-    copy(r("lin"), r("ia", 160, 208))
-    for name, c in (("idn", -1.0), ("idh", 1.0), ("idk", 2048.0), ("idp", 32768.0), ("idm", -BIG), ("idq", BIG)):
+    for name, c in (("idh", 1.0), ("idk", 2048.0), ("idp", 32768.0), ("idm", -BIG), ("idn", -1.0)):
         ts(r(name), r("idb"), c, OP.mult)
-    copy(r("boh"), r("bo", 0, 128))
     ts(r("gw", 0, 8), group, -65536.0, OP.mult)
     ts(r("gw", 8, 16), group, 32768.0, OP.mult)
+    for c, x in enumerate((-1.0, 2.0)):
+        ts(half("bw", c), half("bo", 0), x, OP.mult)
     copy(r("g2", 0, 8), group)
     ts(r("g2", 8, 16), group, -1.0, OP.mult)
-    ts(r("msk"), r("ib", 0, 128), 0.0, OP.is_equal)
-    copy(r("mk2"), r("msk"))
-    fill(r("mk2", 31, 128, 32), 0.0)
-    ts(r("col", 0, 1), row, -1.0, OP.mult, 15.0, OP.add)
-    ts(r("col", 1, 2), row, float(V), OP.add)
-    ts(r("col", 2, 3), row, float(V + 16), OP.add)
-    ts(r("col", 3, 4), row, 15.0, OP.not_equal)
-    for t in (0, 1):
-        ts(r("spare", t, 48, 2), r("one", 0, 24), r("col", 1 + t, 2 + t), OP.mult)
-    copy(r("vl", 0, 16), r("v0s"))
-    ts(r("nzk"), r("nzs"), 16.0, OP.mult, r("col", 0, 1), OP.add)
-    ts(r("wk", 0, 16), r("ib", 128, 144), 0.0, OP.is_equal, 11.0, OP.mult)
-    ts(r("dtab"), r("wk", 0, 16), -3.0, OP.add)
-    fill(r("cut"), 0.0)
-    fill(r("cut", 31, 512, 32), 1.0)
-    for p in range(ST):
-        copy(r("ut", 128 * p, 128 * p + 128, 1, 32), r("msk", 0, 128, 1, 32))
-    fill(r("exa", 0, 512, 1, 32), 3 * BIG)
-    fill(r("one", 0, 256, 1, 32), -1.0)
-    for h in (0, 1):
-        a, b = r("exa", 256 * h, 256 * h + 256, 1, 32), r("exb", 256 * h, 256 * h + 256, 1, 32)
-        select(b, a, [[-16, 2], [0, 4], [1, 32]], OP.is_gt, BIG, 16, -1)
-        select(a, b, [[-16, 2], [0, 4], [1, 32]], OP.not_equal, 0.0, 16, -1)
-        select(r("exa", 256 * h, 256 * h + 256, 1, 16), r("one", 0, 256, 1, 16), [[1, 2], [2, 4], [0, 32]], OP.is_equal, 0.0, 8 * h, -1)
-    copy(r("exh", 0, 512, 1, 32), r("exa", 0, 512, 1, 32))
-    fill(r("exh", 31, 512, 32, 32), 0.0)
+    ts(r("dtab", 0, 16), r("wk", 0, 16), -3.0, OP.add)
+    ts(r("dtab", 16, 32), r("wk", 0, 16), 5.0, OP.add)
+    for e in range(2 * ST):
+        act(r("ut", 128 * e, 128 * e + 128, 1, 32), r("msk", 0, 128, 1, 32), AF.Copy)
+    place[0] = (6.5, 5)
+    act(r("exh", 0, 256, 1, 32), a, AF.Copy)
+    place[0] = None
+    ts(r("nzk"), r("nzs"), 16.0, OP.mult, col(2), OP.add)
 
-    def spread(i):
-        for k in range(16):
-            select(r(zr[i], k, 16 * A, 16), r(zz[i]), [[0, A]], OP.is_ge, 0.0, 0, 0)
+    def spread(i, k):
+        select(r(zr[i], k, 16 * A, 16), r(zz[i]), [[0, A]], OP.is_ge, 0.0, 0, 0)
+
+    def wide_exh(e):
+        a, b = r("exa", 256, 768, 1, 32), r("exb", 256, 768, 1, 32)
+        if e < 2:
+            select(*((a, b) if e else (b, a)), [[0, 2], [-16, 4], [1, 64]], OP.not_equal if e else OP.is_gt, 0.0 if e else BIG, 16, -1)
+        else:
+            select(r("exa", 256, 768, 1, 16), r("exc", 0, 512, 1, 16), [[1, 8], [0, 64]], OP.is_equal, 0.0, 0, -1)
+            act(r("exh", 256, 768, 1, 32), a, AF.Copy)
+
+    later = [(wide_exh, e) for e in range(3)] + [(lambda k: spread(2, k), k) for k in range(16)]
 
     def ish(j):
         return j // 6, (j % 6) // 2, 1 - j % 2
 
     def nodes(slot, h):
-        return r("vl", 16 * slot + 8 * h, 16 * slot + 8 * h + 8)
-
-    def keys(h):
-        return r("kb%d" % h, 0, 128)
+        return half("vl", 8 * (slot // 4) + 4 * h + slot % 4, 8)
 
     def cuts(a, b, most):
         m = -(-(b - a) // most)
@@ -371,165 +410,197 @@ def rank_program(g, core, T, topo):
 
     def half_step(j):
         i, s, h = ish(j)
-        na, nb, late, kb = NA[j], NB[j], j in (12, 13), "kb%d" % h
+        kb, a = "kb%d" % h, 128 * h + 3 * i + s
+        keys = r(kb, 0, 128)
         wide = lambda name, a, b: r(name, 16 * (128 * h + a), 16 * (128 * h + b))
         feats = lambda a, b: ind(r("xs"), r("nm", 128 * h + a, 128 * h + b))
         at(j, "names", copy, half("nm", h), ind(r("adjs"), nodes(4 * i + s, h)))
         at(j, "centred", ts, half("ee", h), half("nm", h), float(-OFF), OP.add)
-        at(j, "open", mm, keys(h), half("ee", h), r("idh"), True, False)
-        for t, (a, b) in enumerate(cuts(128 - nb, 128, AC)):
+        at(j, "open", mm, keys, r("nzk", a, a + 128), r("idk"), True)
+        cut = CUT[KIND[j]]
+        na, nc = cut[0] + cut[1], sum(cut[:3])
+        for t, (a, b) in enumerate([(nc, nc + min(AC, cut[3]))] + cuts(nc + min(AC, cut[3]), 128, AC)):
             sb = r("sb%d" % (bank[0] % 3), 0, 16 * (b - a))
             bank[0] += 1
-            at(j, "ag%d" % t, act, wide("dd", a, b), feats(a, b), AF.Copy)
-            at(j, "sz%d" % t, mm, sb, r("idn"), wide(zr[i], a, b), True, False)
-            at(j, "sg%d" % t, mm, sb, r("idb"), wide("dd", a, b), False, True)
-            at(j, "aa%d" % t, act, wide("rr", a, b), sb, AF.Abs, 0.5)
-        for t, (a, b) in enumerate(cuts(na, 128 - nb, VC)):
-            at(j, "vc%d" % t, tt, wide("dd", a, b), feats(a, b), wide(zr[i], a, b), OP.subtract)
-        for t, (a, b) in enumerate(cuts(na, 128 - nb, CC)):
-            at(j, "ca%d" % t, act, wide("rr", a, b), wide("dd", a, b), AF.Abs, 0.5)
-        for t, (a, b) in enumerate(cuts(0, na, VC)):
-            at(j, "va%d" % t, tt, wide("dd", a, b), feats(a, b), wide(zr[i], a, b), OP.subtract)
-        if na:
-            at(j, "relu", ts, wide("rr", 0, na), wide("dd", 0, na), 0.0, OP.max)
-            for k in range(16):
-                at(j, "sumd", mm, r(kb, k, 128, 16, na), r("dd", 2048 * h + k, 2048 * h + 16 * na, 16), r("gw", 8, 16), False, False)
-        a = 128 * h + 3 * i + s
-        at(j, "noise", mm, keys(h), r("nzk", a, a + 128), r("idk"), False, False)
-        if i == 2 and not late:
-            at(j, "ag0", act, half("phg", h), ind(r("ph"), nodes(4 * i + s, h)), AF.Copy)
-            at(j, "noise", mm, keys(h), half("phg", h), r("idp"), False, False)
+            at(j, "g%d" % t, act, wide("dd", a, b), feats(a, b), AF.Copy)
+            at(j, "z%d" % t, mm, sb, r("idn"), wide(zr[i], a, b), True)
+            at(j, "x%d" % t, mm, sb, r("idb"), wide("dd", a, b), False)
+            at(j, "a%d" % t, act, wide("rr", a, b), sb, AF.Abs, 0.5)
+        for t in range(3):
+            a, b = sum(cut[:t]), sum(cut[:t + 1])
+            if b > a:
+                at(j, "v%d" % t, tt, wide("dd", a, b), feats(a, b), wide(zr[i], a, b), OP.subtract)
+                if t < 2:
+                    at(j, "relu%d" % t, ts, wide("rr", a, b), wide("dd", a, b), 0.0, OP.max)
+                else:
+                    at(j, "abs", act, wide("rr", a, b), wide("dd", a, b), AF.Abs, 0.5)
+        for k in range(16 if na else 0):
+            at(j, "sumd", mm, r(kb, k, 128, 16, na), r("dd", 2048 * h + k, 2048 * h + 16 * na, 16), r("gw", 8, 16), False)
+        at(j, "name", mm, keys, half("ee", h), r("idh"), False)
+        if j >= 14:
+            at(j, "ph0", act, half("phg", h), ind(r("ph"), nodes(4 * i + s, h)), AF.Copy)
+            at(j, "name", mm, keys, half("phg", h), r("idp"), False)
         for k in range(16):
-            at(j, "sumr", mm, r(kb, k, 128, 16), r("rr", 2048 * h + k, 2048 * h + 2048, 16), r("gw", 0, 8), False, k == 15 and not late)
+            at(j, "sum", mm, r(kb, k, 128, 16), r("rr", 2048 * h + k, 2048 * h + 2048, 16), r("gw", 0, 8), False)
 
     def choice(j):
         i, s, h = ish(j)
         kb = "kb%d" % h
+        keys = r(kb, 0, 128)
         if j in (12, 13):
             at(j, "ph", act, half("phg", h), ind(r("ph"), nodes(4 * i + s, h)), AF.Copy)
-            at(j, "phk", mm, keys(h), half("phg", h), r("idp"), False, True)
-        at(j, "best", scan, half("sc", h), r("rst"), keys(h), 0.0, OP.add, OP.max)
+            at(j, "close", mm, keys, half("phg", h), r("idp"), False)
+        at(j, "best", scan, half("sc", h), r("rst"), keys, 0.0, OP.add, OP.max)
         at(j, "widen", tt, half("ll", h), ind(half("sc", h), r("bc")), r("msk"), OP.mult)
-        right = r(kb, 152 + s, 176, 3)
-        at(j, "turn", mm, r(kb, 128 + s, 176, 3), half("ll", h), r("g2"), True, False)
-        at(j, "turn", mm, right, r("idb"), r("mg", 0, 8), False, False)
-        at(j, "turn", mm, right, r("idb"), r("mg", 8, 16), False, False)
-        at(j, "turn", mm, right, half("ll", h), r("g2", 0, 8), False, True)
-        at(j, "chosen", ts, nodes(4 * i + s + 1, h), right, float(OFF), OP.add)
+        right = r(kb, 408 + s, 432, 3)
+        at(j, "turn", mm, r(kb, 384 + s, 432, 3), half("ll", h), r("g2"), True)
+        at(j, "turn", mm, right, r("idb"), r("mg", 0, 8), False)
+        at(j, "turn", mm, right, r("idb"), r("mg", 8, 16), False)
+        at(j, "turn", mm, right, half("ll", h), r("g2", 0, 8), False)
+        if s == ST - 1 and "chosenv" in [k for k, d in ORDER["V"]]:
+            at(j, "chosenv", ts, nodes(4 * i + s + 1, h), right, float(OFF), OP.add)
+        else:
+            at(j, "chosen", act, nodes(4 * i + s + 1, h), right, AF.Identity, 1.0, float(OFF))
         if s == ST - 1:
             if i < VIS - 1:
                 post(nxt, nodes(4 * i + 4, h), nodes(4 * i + 3, h), "a_v%d%d" % (i + 1, h))
-            distance(i, h)
-            if i < VIS - 1:
-                ts(half("ki", h, 24), r(kb, 128, 152), float(OFF), OP.add)
+                ts(half("ki", h, 24), r(kb, 384, 408), float(OFF), OP.add)
+            distance(j)
 
-    def distance(i, h):
+    def distance(j):
+        i, s, h = ish(j)
         far = r("kb%d" % h, 256, 384)
-        tt(half("fd", h), ind(r("xs"), nodes(4 * i + 3, h)), half(zz[i], h), OP.subtract)
-        act(half("fa", h), half("fd", h), AF.Abs)
-        mm(far, r("bo", 0, 128), half("fa", h), True, True)
+        at(j, "end", tt, half("fd", h), ind(r("xs"), nodes(4 * i + 3, h)), half(zz[i], h), OP.subtract)
+        at(j, "endabs", ts, half("fa", h), half("fd", h), 0.0, OP.max)
+        at(j, "far", mm, far, half("bw", 0), half("fd", h), True)
+        at(j, "far", mm, far, half("bw", 1), half("fa", h), False)
         if i > 0:
-            tt(half("fo%d" % i, h), far, half("di%d" % (i - 1), h), OP.is_lt)
+            at(j, "flag", tt, half("fo%d" % i, h), far, half("di%d" % (i - 1), h), OP.is_lt)
             post(prv, half("fi%d" % i, h), half("fo%d" % i, h), "a_f%d%d" % (i, h))
         if i < VIS - 1:
             act(half("do%d" % i, h), far, AF.Copy)
 
-    def trail(i):
-        w, nn, pp, ex = [lambda t, name=name: half(name, t, 16) for name in ("wk", "nn", "pp", "ex")]
-        yy, ud = r("yy%d" % i), r("ud%d" % i)
-        copy(r("vf"), r("vl", 64 * i, 64 * i + 64))
-        ts(r("kb"), r("ki"), 15 << 11, OP.bitwise_and)
-        tt(r("nn", 0, 48), r("vf", 0, 48), r("vf", 16, 64), OP.not_equal)
-        tt(r("nn", 48, 80), r("vf", 0, 32), r("vf", 32, 64), OP.not_equal)
-        tt(ex(0), r("vf", 0, 16), r("vf", 48, 64), OP.not_equal)
+    def trail(i, h):
+        def part(name, slots):
+            return lambda a=0, b=None: r(name, 8 * (slots * h + a), 8 * (slots * h + (a + 1 if b is None else b)))
+        vf, nn, w = part("vf", 4), part("nn", 5), part("wk", 11)
+        pp, ex, kb, un, kr, y0, ku, uh, yy, ul = [part(x, 3) for x in ("pp", "ex", "kb", "un", "kr", "y0", "ku", "uh", "yy%d" % i, "ul%d" % i)]
+        copy(vf(0, 4), r("vl", 64 * i + 32 * h, 64 * i + 32 * h + 32))
+        ts(kb(0, 3), half("ki", h, 24), 15 << 11, OP.bitwise_and)
+        tt(nn(0, 3), vf(0, 3), vf(1, 4), OP.not_equal)
+        tt(nn(3, 5), vf(0, 2), vf(2, 4), OP.not_equal)
+        tt(ex(0), vf(0), vf(3), OP.not_equal)
         for s in range(ST):
-            tt(pp(s), r("kb", s, 48, 3), half("vf", s, 16), OP.add)
+            tt(pp(s), r("kb", 24 * h + s, 24 * h + 24, 3), vf(s), OP.add)
         tt(w(2), nn(0), nn(3), OP.mult)
         tt(w(3), nn(0), nn(1), OP.mult)
         tt(w(7), nn(3), nn(4), OP.mult)
-        tt(r("wk", 0, 32), r("pp", 16, 48), r("pp", 0, 32), OP.subtract)
+        tt(w(0, 2), pp(1, 3), pp(0, 2), OP.subtract)
         tt(w(9), nn(0), nn(2), OP.max)
         tt(w(10), w(3), nn(2), OP.mult)
         tt(w(8), w(7), ex(0), OP.mult)
-        tt(r("wk", 64, 96), r("wk", 32, 64), r("wk", 0, 32), OP.mult)
+        tt(w(4, 6), w(2, 4), w(0, 2), OP.mult)
         tt(w(6), nn(3), w(1), OP.mult)
-        tt(ex(1), w(8), w(9), OP.mult)
+        tt(ex(1, 3), r("wk", 88 * h + 72, 88 * h + 88), r("wk", 88 * h + 64, 88 * h + 80), OP.min)
+        tt(ex(2), ex(1), ex(2), OP.min)
         tt(pp(1), pp(2), w(5), OP.subtract)
         tt(w(7), w(4), w(6), OP.add)
-        tt(ex(2), w(8), w(10), OP.mult)
         tt(pp(0), pp(2), w(7), OP.subtract)
-        ts(r("un"), r("pp"), 2047, OP.bitwise_and)
-        ts(r("kr"), r("pp"), 11, OP.arith_shift_right)
-        tt(r("y0"), r("un"), r("spare"), OP.subtract)
-        copy(r("ku%d" % i), r("kr"))
-        tt(yy, r("y0"), r("ex"), OP.mult)
-        tt(ud, yy, r("spare"), OP.add)
-        copy(r("ul%d" % i), ud)
-        copy(r("uh%d" % i), ud)
-        act(r("dl%d" % i), ind(r("dtab"), r("ku%d" % i)), AF.Copy)
+        ts(un(0, 3), pp(0, 3), 2047, OP.bitwise_and)
+        ts(kr(0, 3), pp(0, 3), 11, OP.arith_shift_right)
+        tt(y0(0, 3), r("spare"), un(0, 3), OP.subtract)
+        copy(ku(0, 3), kr(0, 3))
+        tt(yy(0, 3), y0(0, 3), ex(0, 3), OP.mult)
+        tt(uh(0, 3), r("spare"), yy(0, 3), OP.subtract)
+        copy(ul(0, 3), uh(0, 3))
+        if i == 0:
+            act(half("tc", h), ind(r("dtab", 16, 32), ku(0)), AF.Copy)
+        act(r("dl%d" % i, 384 * h + 128 * (1 - i), 384 * h + 384), ind(r("dtab", 0, 16), ku(1 - i, 3)), AF.Copy)
 
-    def region(p, h, a=0, b=256, step=1):
-        name, c = ("px%d" % h, 256 * p) if p < 2 else ("pz", 256 * h)
-        return r(name, c + a, c + b, step)
-
-    def differences(i):
+    def turned(i, h):
+        sb = "sb%d" % (bank[0] % 3)
+        bank[0] += 1
         for p in range(ST):
-            mm(r("pz", 128 * p, 128 * p + 128, 1, 16), half("uh%d" % i, p, 16), r("idh"), True, True)
-        copy(r("ut", 0, 384, 1, 16), r("pz", 0, 384, 1, 16))
-        for e in range(6):
-            tt(half("um", e), ind(r("ud%d" % i), half("lin", e, 8)), r("mk2"), OP.mult)
-        for p, h in ((0, 1), (1, 1), (0, 0), (1, 0), (2, 1), (2, 0)):
-            mm(region(p, h), r("ut", 128 * p, 128 * p + 128, 1, 32), r("exh", 256 * h, 256 * h + 256, 1, 32), p == 0 or (p, h) == (2, 1), False)
-            for t in (0, 1):
-                mm(region(p, h, 128 * t, 128 * t + 128), r("boh"), half("um", 2 * p + h), False, False)
+            mm(r(sb, 128 * p, 128 * p + 128, 1, 8), half("uh", 3 * h + p, 8), r("idh"), True)
+        act(r("ut", 384 * h, 384 * h + 384, 1, 8), r(sb, 0, 384, 1, 8), AF.Copy)
+        act(half("um", h, 384), ind(r("num"), half("ul%d" % i, h, 24)), AF.Copy, 1.0 / 16)
 
-    def renewed(i, p):
-        tt(r("tm"), ind(r("ph"), half("ul%d" % i, p, 16)), half("dl%d" % i, p, 256), OP.add)
-        ts(r("tc"), r("tm"), 0.0, OP.max, 20.0, OP.min)
+    def spread_over(p, lhsT, name, c):
+        if p == 0:
+            for t in (0, 1):
+                mm(half("px0", t), lhsT, r(name, c, c + 128), False)
+        else:
+            for e in range(8):
+                mm(half("px%d" % p, e, 64), lhsT, r(name, c + 64 * (e // 4), c + 64 * (e // 4) + 64), False)
+
+    def differences(h):
+        for p in range(ST):
+            c, (a, m) = 384 * h + 128 * p, ((256, 512) if p else (0, 256))
+            mm(r("px%d" % p, 0, m), r("ut", c, c + 128, 1, 32), r("exh", a, a + m, 1, 32), True)
+            spread_over(p, r("idh"), "um", c)
+
+    def winners(i, h):
+        for p in range(ST):
+            c, m = 1280 * h + 512 * p - 256 * (p > 0), 512 if p else 256
+            spread_over(p, r("idm"), "fi%d" % (i + 1), 128 * h)
+            act(r("ab", c, c + m), r("px%d" % p, 0, m), AF.Abs, BIG)
+            scan(r("pr", c, c + m), r("rs2", 256 * (p > 0), 256 * (p > 0) + m), r("ab", c, c + m), 0.0, OP.add, OP.min)
+        for t in (0, 1):
+            mine = lambda name: r(name, 24 * h + t, 24 * h + 8, 2)
+            tt(mine("ok"), r("pr", 1280 * h + 128 * t + 31, 1280 * h + 128 * t + 128, 32), mine("yy%d" % i), OP.min)
+            ts(mine("lst"), mine("ok"), -1.0, OP.mult, r("spare", t, t + 1), OP.add)
+        for p0, p1 in ((1, 3),) if h else ((1, 2), (2, 3)):
+            mine = lambda name: r(name, 24 * h + 8 * p0, 24 * h + 8 * p1)
+            tt(mine("ok"), r("pr", 1280 * h + 512 * p0 - 256 + 63, 1280 * h + 512 * p1 - 256, 64), mine("yy%d" % i), OP.min)
+            tt(mine("lf"), r("spare", 8 * p0, 8 * p1), mine("ok"), OP.subtract)
+            copy(mine("lst"), mine("lf"))
+
+    def renewed(i, p, halves=(1, 0)):
+        for h in halves:
+            tt(half("tm", h), ind(r("ph"), half("ul%d" % i, 3 * h + p, 8)), half("dl%d" % i, 3 * h + p), OP.add)
+        for h in halves:
+            ts(half("tc", h), half("tm", h), 0.0, OP.max, 20.0, OP.min)
 
     def reinforce(i):
-        fi, yy = "fi%d" % (i + 1), "yy%d" % i
-        for h in (1, 0):
-            ts(r("cut", 256 * h + 127, 256 * h + 255, 32), r(fi, 128 * h + 31, 128 * h + 128, 32), r("col", 3, 4), OP.max)
-        for pair in (((0, 1), (1, 1)), ((0, 0), (1, 0)), ((2, 1), (2, 0))):
-            for p, h in pair:
-                for t in (0, 1):
-                    mm(region(p, h, 128 * t, 128 * t + 128), r("idm"), half(fi, h), False, False)
-                    mm(region(p, h, 128 * t + 31, 128 * t + 128, 32), r("idq"), r(fi, 128 * h + 31, 128 * h + 128, 32), False,
-                       t == 1 and (p, h) == pair[1])
-            for p, h in pair:
-                e, c = 2 * p + h, 16 * p + 8 * h
-                act(half("ab", e, 256), region(p, h), AF.Abs)
-                scan(half("pr", e, 256), half("ab", e, 256), half("cut", h, 256), 1.0, OP.min, OP.max)
-                for t in (0, 1):
-                    tt(r("ok", c + t, c + 8, 2), r("pr", 256 * e + 128 * t + 30, 256 * e + 128 * t + 128, 32), r(yy, c + t, c + 8, 2), OP.mult)
-                    ts(r("lst", c + t, c + 8, 2), r("ok", c + t, c + 8, 2), r("col", 1 + t, 2 + t), OP.add)
+        winners(i, 1)
+        differences(0)
+        winners(i, 0)
         for p in range(ST):
             if p > 0:
                 renewed(i, p)
-            for j in range(7, -1, -1):
-                copy(ind(r("ph"), r("lst", 16 * p + 2 * j, 16 * p + 2 * j + 2)), r("tc", 32 * j, 32 * j + 32))
+            m = 4 if p else 2
+            for c in range(16 - m, -1, -m):
+                e = 24 * (c // 8) + 8 * p + c % 8
+                copy(ind(r("ph"), r("lst", e, e + m)), r("tc", 16 * c, 16 * (c + m)))
 
-    spread(1)
-    post(two, r("z2"), r("z0"), "a_z2")
+    for k in range(16):
+        spread(1, k)
+    for fn, e in later[:NUM["early"]]:
+        fn(e)
     for i in range(VIS):
         for j in range(6 * i, 6 * i + 6):
             half_step(j)
             if j == 13:
                 reinforce(0)
-                differences(1)
                 renewed(1, 0)
                 choice(12)
             if j != 12:
                 choice(j)
+            for e in (0, 1):
+                for h in (1, 0):
+                    if j == NUM["turn%d%d" % (e, h)]:
+                        turned(e, h)
+                        if h:
+                            differences(1)
+            if j in (4, 5, 10, 11):
+                trail(i, 1 - j % 2)
         if i < VIS - 1:
             post(nxt, r("di%d" % i), r("do%d" % i), "a_d%d" % i)
-            trail(i)
         if i == 0:
-            spread(2)
-            differences(0)
-            renewed(0, 0)
-    copy(r("yvs"), r("vl", 176, 192))
+            for fn, e in later[NUM["early"]:]:
+                fn(e)
+    for h in (1, 0):
+        copy(half("yvs", h, 8), nodes(11, h))
     dma(T.yv[:], r("yvs"), "s_yv", 2500)
     reinforce(1)
     dma(T.yp[:], r("ph", 0, V), "s_yp", 4000)

import numpy as np
from concourse.mybir import AluOpType as OP, ActivationFunctionType as AF

V, A, VIS, ST = 1888, 256, 3, 3
PW = V + 64
OFF = 944
MAG = 1.5 * 2.0 ** 34
BIG = 4096.0
H16, B16, F32, I32, U16 = "float16", "bfloat16", "float32", "int32", "uint16"

KIND = "abbbbz" "accccz" "degffz"
AC = 32
STEP = {"late": 0.25, "shift": 0.25, "early": 1, "look": 30, "slack": 50, "turn01": 1, "turn00": 1, "turn11": 1, "turn10": 1, "flag": 0.05,
        "far": 0.05, "runs": 0}
TAIL = ("ph", "close", "best", "widen", "turn", "chosen")
FLAG = ("end", "endabs", "far", "flag")
SOLO = {"v2": "v1", "abs": "a1"}
RUNS = [[range(18)],
        [range(0, 6), range(6, 12), [12], [13], range(14, 18)],
        [[0], range(1, 6), [6], range(7, 12), [12], [13], [14], range(15, 18)],
        [range(0, 6), range(6, 12), range(12, 18)],
        [range(0, 12), [12], [13], range(14, 18)]]
ORDER, CUT, NUM = ({'V': [('v2', 0), ('v0', 0), ('centred', 0), ('best', -1), ('relu0', 0), ('widen', -1), ('v1', 0), ('end', -1), ('endabs', -1), ('names', 1), ('relu1', 0), ('flag', -1)], 'A': [('a0', -1), ('chosen', -2), ('a1', -1), ('ph0', 0), ('ph', 0), ('g0', 0), ('a2', -1), ('g2', 0), ('g1', 0), ('abs', 0)], 'P': [('sumd', -1), ('name', -1), ('far', -2), ('sum', -1), ('z1', 0), ('z2', 0), ('x0', 0), ('x1', 0), ('x2', 0), ('turn', -1), ('open', 0), ('z0', 1), ('close', 0)]}, {'a': (16, 50, 14, 30), 'g': (26, 46, 0, 34), 'b': (18, 36, 18, 28), 'c': (20, 38, 14, 46), 'd': (38, 20, 0, 56), 'e': (22, 6, 12, 34), 'f': (16, 40, 20, 40), 'z': (28, 20, 16, 32)}, {'late': 3.0, 'shift': 0.75, 'early': 1, 'look': 30, 'slack': 350, 'turn01': 7, 'turn00': 11, 'turn11': 13, 'turn10': 17, 'flag': 0.15, 'far': 0.3, 'runs': 4})
PHI, GAT, SCA, CY, PE, ACT0 = 1.25, 1.56, 3.8, 0.833, 0.417, 64
WAKE, SAME, FAR, FIRST = 140, 140, 2400, 3000

SB = {
    "adjs": (V, I32), "xs": (V, B16), "z0": (A, B16), "z1": (A, B16), "z2": (A, B16),
    "zr0": (16 * A, B16), "zr1": (16 * A, B16), "zr2": (16 * A, B16), "nzs": (A + 8, B16), "nzk": (A + 8, H16),
    "v0s": (16, I32), "vl": (12 * 16, U16), "nm": (A, U16), "ee": (A, H16), "phg": (A, B16),
    "dd": (16 * A, B16), "rr": (16 * A, B16), "ph": (PW, B16), "num": (PW, F32), "sc": (A, F32), "ll": (A, F32), "fd": (A, B16), "fa": (A, B16),
    "do0": (A, B16), "do1": (A, B16), "di0": (A, B16), "di1": (A, B16), "fo1": (A, B16), "fo2": (A, B16), "fi1": (A, B16), "fi2": (A, B16),
    "ia": (176, I32), "ib": (144, I32), "one": (128, B16), "idb": (128, B16), "idn": (128, B16), "idp": (128, B16),
    "idm": (128, B16), "idh": (128, H16), "idk": (128, H16), "bo": (256, B16), "bw": (256, B16),
    "gw": (16, B16), "g2": (16, F32), "mg": (16, B16), "msk": (128, F32), "rst": (128, F32), "rs2": (768, B16),
    "bc": (8, U16), "dtab": (32, B16), "col": (4, F32), "spare": (24, F32), "lf": (48, F32),
    "exa": (768, B16), "exb": (768, B16), "exc": (512, B16), "exh": (768, H16), "ut": (768, H16), "um": (768, H16), "yy0": (48, F32), "yy1": (48, F32),
    "vf": (64, F32), "ki": (48, I32), "kb": (48, I32), "pp": (48, I32), "nn": (80, F32), "ex": (48, F32), "wk": (176, F32),
    "un": (48, I32), "kr": (48, I32), "y0": (48, F32), "ku": (48, U16), "uh": (48, H16), "ul0": (48, U16), "ul1": (48, U16),
    "dl0": (768, B16), "dl1": (768, B16), "ab": (2560, B16), "pr": (2560, B16), "ok": (48, F32), "lst": (48, U16),
    "tm": (A, B16), "tc": (A, B16), "yvs": (16, F32),
}
SCRATCH = {k: ("sbuf", [128, w], d) for k, (w, d) in SB.items()}
SCRATCH.update({k: ("psum", [128, 512], F32) for k in ("kb0", "kb1", "sb0", "sb1", "sb2", "px0", "px1", "px2")})
ARRIVALS = ["a_z1", "a_z2", "a_v10", "a_v11", "a_v20", "a_v21", "a_d0", "a_d1", "a_f10", "a_f11", "a_f20", "a_f21"]
LOADS = ["l_adj", "l_x", "l_z", "l_v", "l_nz", "l_nw", "s_yv", "s_yp"]
ENG = ("sV", "sA", "sP", "sG")
SEMAPHORES = list(ENG) + ["sent"] + ARRIVALS + LOADS
PLAN = []
SPAN = [0]
SEEN = {}


def view(name, parts, *ix):
    key = (name, tuple((s.start, s.stop, s.step) for s in ix))
    if key not in SEEN:
        shape = SCRATCH[name][1][1:]
        el = np.arange(int(np.prod(shape))).reshape(shape)[ix].reshape(-1)
        SEEN[key] = (sum(1 << int(e) for e in el), len(el))
    return ("r", name, (slice(*parts) if isinstance(parts, tuple) else slice(0, parts),) + ix) + SEEN[key]


def r(name, a=0, b=None, step=1, parts=128):
    if len(SCRATCH[name][1]) == 3:
        return view(name, parts, slice(None), slice(None))
    return view(name, parts, slice(a, SCRATCH[name][1][1] if b is None else b, None if step == 1 else step))


def ind(win, off):
    return ("i", win, off)


def links(ops):
    hist, hard, soft, last = {}, [], [], {}
    for i, (q, sem, inc, reads, writes, emit, cost, tag) in enumerate(ops):
        hd, sf = set(), set()
        acc = [(x, False) for x in reads] + [(x, True) for x in writes]
        for x, wr in acc:
            psum = SCRATCH[x[1]][0] == "psum"
            for j, y, wr2 in hist.get(x[1], []):
                if psum:
                    (sf if ops[j][0] == q else hd).add(j)
                elif (wr or wr2) and ops[j][1] is not None and x[3] & y[3]:
                    hd.add(j)
        if q in "GS":
            if q in last:
                sf.add(last[q])
            last[q] = i
        for x, wr in acc:
            h = hist.setdefault(x[1], [])
            if SCRATCH[x[1]][0] == "psum":
                h[:] = [e for e in h if ops[e[0]][0] != q]
            elif wr and x[2][0].stop == 128:
                h[:] = [e for e in h if e[1][3] & ~x[3]]
            h.append((i, x, wr))
        hard.append(hd - {i})
        soft.append(sf - {i})
    for q in ORDER:
        for run in RUNS[NUM["runs"]]:
            chain = sorted((o[7], i) for i, o in enumerate(ops) if o[0] == q and o[7] is not None and o[7][1] in run)
            for (_, a), (_, b) in zip(chain, chain[1:]):
                soft[b].add(a)
    return hard, soft


def arrange(ops, hard, soft):
    n = len(ops)
    sender = {o[7]: i for i, o in enumerate(ops) if o[1] is None}
    pre = []
    for i, o in enumerate(ops):
        p = [(j, ops[j][6][1] + (SAME if ops[j][0] == o[0] else WAKE)) for j in hard[i]] + [(j, ops[j][6][0]) for j in soft[i]]
        if o[0] == "X":
            p.append((sender[o[1]], FAR))
        pre.append(p)
    after = [[] for _ in ops]
    for i, p in enumerate(pre):
        for j, d in p:
            after[j].append((i, d))
    left = [len(p) for p in pre]
    line = [i for i in range(n) if not left[i]]
    for i in line:
        for j, d in after[i]:
            left[j] -= 1
            if not left[j]:
                line.append(j)
    assert len(line) == n
    rest = [0.0] * n
    for i in reversed(line):
        rest[i] = max([ops[i][6][1]] + [d + rest[j] for j, d in after[i]])
    left = [len(p) for p in pre]
    ready = [0.0] * n
    free = {}
    cand = [i for i in range(n) if not left[i]]
    order = []
    while cand:
        t, q = min((max(ready[i], free.get(ops[i][0], 0.0)), ops[i][0]) for i in cand)
        mine = sorted((k for k in cand if ops[k][0] == q), key=lambda k: (-rest[k], k))
        i = None
        for m, k in enumerate(mine):
            if ready[k] <= t + NUM["look"] and all(t + ops[k][6][0] <= ready[u] + NUM["slack"] for u in mine[:m] if rest[u] > rest[k] + 300):
                i = k
                break
        if i is None:
            i = min(mine, key=lambda k: (max(ready[k], t) - rest[k], k))
            other = [max(ready[k], free.get(ops[k][0], 0.0)) for k in cand if ops[k][0] != q]
            if other and min(other) < ready[i]:
                free[q] = min(other) + 1.0
                continue
        t = max(t, ready[i])
        free[q] = t + ops[i][6][0]
        cand.remove(i)
        order.append(i)
        for j, d in after[i]:
            ready[j] = max(ready[j], t + d)
            left[j] -= 1
            if not left[j]:
                cand.append(j)
    SPAN[0] = max(free.values())
    return order


def plan_waits(ops, hard, order):
    total, clock, done, out = {}, {}, {}, {}
    for i in order:
        q, sem, inc = ops[i][:3]
        need = {}
        for j in hard[i]:
            s, c, k = done[j]
            if need.get(s, (0, None))[0] < c:
                need[s] = (c, k)
        ck = clock.setdefault(q, {})
        waits = []
        for s, (c, k) in sorted(need.items(), key=lambda e: (-sum(e[1][1].values()), e[0])):
            if ck.get(s, 0) < c:
                waits.append((s, c))
                for s2, c2 in k.items():
                    if ck.get(s2, 0) < c2:
                        ck[s2] = c2
        if sem is not None:
            total[sem] = total.get(sem, 0) + inc
            k = dict(ck)
            k[sem] = total[sem]
            done[i] = (sem, total[sem], k)
        out[i] = waits
    return out, total


def rank_program(g, core, T, topo):
    rank = T.rank_of(core)
    if rank is None:
        return
    n = len(T.cores)
    nxt, prv, two = T.cores[(rank + 1) % n], T.cores[(rank - 1) % n], T.cores[(rank + 2) % n]
    engines = topo.mask(core, nxt) & topo.mask(core, prv) & topo.mask(core, two)
    width = bin(engines).count("1")
    Q = {"V": g.vector, "A": g.scalar, "P": g.tensor, "G": g, "S": g.sync}
    ops, posts, place, adding = [], [], [None], {}

    def at(j, kind, fn, *args):
        slot = j + NUM["shift"] * (j // 6) + (NUM["late"] if j >= 14 or (j >= 12 and kind in TAIL) else 0)
        if j == 1 and kind == "names":
            slot = 0.01
        like = SOLO.get(kind, kind) if KIND[j] in "ag" else kind
        place[0] = [slot - d + m / len(o) for o in ORDER.values() for m, (k, d) in enumerate(o) if k == like][0] + 0.001 * (like != kind)
        if j == 11 and kind in FLAG:
            place[0] = 12 + 2 * NUM["shift"] + NUM["far" if kind == "far" else "flag"] + 0.001 * FLAG.index(kind)
        place[0] = (place[0], j)
        fn(*args)
        place[0] = None

    def ap(x):
        if not isinstance(x, tuple):
            return x
        if x[0] == "i":
            return ap(x[1]).indirect(ap(x[2]))
        return T[x[1]][x[2]]

    def count(x):
        return 16 * x[2][4] if x[0] == "i" else x[4]

    def price(q, out, ins, sem, per):
        if sem:
            return (50, per)
        m = count(out)
        wide = [x for x in [out] + ins if isinstance(x, tuple) and count(x) > 1]
        if any(x[0] == "i" for x in wide):
            d = (50 if q == "V" else 65) + m * CY * (SCA if out[0] == "i" else GAT)
        elif q == "P":
            d = 5 + max(min(64, count(ins[0])), m) * PE * PHI * (4 if SCRATCH[ins[0][1]][2] == F32 else 1)
        elif q == "G":
            d = (170 + 2 * m * CY) * PHI
        elif q == "A":
            d = (ACT0 + m) * CY * PHI
        else:
            if per == 1.0 and all(SCRATCH[x[1]][2] in (B16, H16, U16) for x in wide):
                per = 0.5
            if per == 2.0 and any(SCRATCH[x[1]][0] == "psum" for x in wide):
                per = 1.0
            d = max(64, m * per) * CY * PHI
        return (d, d)

    def add(q, fn, out, ins, sem=None, inc=1, per=1.0):
        reads, writes = [], []
        for x in ins:
            if isinstance(x, tuple):
                reads += [x[1], x[2]] if x[0] == "i" else [x]
        if isinstance(out, tuple):
            if out[0] == "i":
                writes.append(out[1])
                reads.append(out[2])
            else:
                writes.append(out)
        ops.append([q, sem or "s" + q, inc, reads, writes, fn, price(q, out, ins, sem, per), place[0]])
        for x in reads:
            adding.pop(x[1], None)

    def copy(out, in_):
        add("V", lambda: g.vector.tensor_copy(ap(out), ap(in_)), out, [in_])

    def tt(out, a, b, op):
        add("V", lambda: g.vector.tensor_tensor(ap(out), ap(a), ap(b), op), out, [a, b], per=2.0)

    def ts(out, a, s1, op0, s2=None, op1=None):
        if op1 is None:
            add("V", lambda: g.vector.tensor_scalar(ap(out), ap(a), ap(s1), None, op0), out, [a, s1])
        else:
            add("V", lambda: g.vector.tensor_scalar(ap(out), ap(a), ap(s1), ap(s2), op0, op1), out, [a, s1, s2])

    def fill(out, c):
        add("V", lambda: g.vector.memset(ap(out), c), out, [])

    def scan(out, d0, d1, init, op0, op1):
        add("V", lambda: g.vector.tensor_tensor_scan(ap(out), ap(d0), ap(d1), init, op0, op1), out, [d0, d1])

    def act(out, in_, func, scale=1.0, bias=0.0):
        add("A", lambda: g.scalar.activation(ap(out), ap(in_), func, bias=ap(bias), scale=ap(scale)), out, [in_, scale, bias])

    def mm(out, lhsT, rhs, start):
        ends = [True]
        add("P", lambda: g.tensor.matmul(ap(out), ap(lhsT), ap(rhs), start, ends[0]), out, [lhsT, rhs])
        if not start and adding.get(out[1]):
            adding[out[1]][0] = False
        adding[out[1]] = ends

    def iota(out, pattern, base, cm):
        add("G", lambda: g.iota(ap(out), pattern, base, cm), out, [])

    def select(out, in_, pattern, op, c, base, cm):
        add("G", lambda: g.affine_select(ap(out), ap(in_), pattern, op, c, base, cm), out, [in_])

    def dma(out, in_, sem, when):
        add("S", lambda: g.sync.dma_start(ap(out), ap(in_)), out, [in_], sem, 16, when)

    def post(dst, out, in_, sem):
        rid, pid = topo.addr(dst, core)
        ops.append(["G", None, 0, [in_], [],
                    lambda: g.remote_dma(ap(out), ap(in_), T.sem[sem], T.sem.sent, pid, rid, engines),
                    (300, 300) if posts else (FIRST, FIRST), sem])
        posts.append(sem)

    def landed(buf, sem):
        ops.append(["X", sem, width, [], [buf], None, (0, 0), None])

    def half(name, h, per=128):
        return r(name, per * h, per * h + per)

    def col(c):
        return r("col", c, c + 1)

    zz, zr = ["z0", "z1", "z2"], ["zr0", "zr1", "zr2"]
    for i in (1, 2):
        landed(r(zz[i]), "a_z%d" % i)
        landed(r("di%d" % (i - 1)), "a_d%d" % (i - 1))
        for h in (0, 1):
            landed(half("vl", 8 * i + 4 * h, 8), "a_v%d%d" % (i, h))
            landed(half("fi%d" % i, h), "a_f%d%d" % (i, h))

    dma(r("z0"), T.z[:], "l_z", 2300)
    dma(r("v0s"), T.v0[:], "l_v", 2300)
    dma(r("adjs"), T.adj[:], "l_adj", 6100)
    dma(r("xs"), T.x[:], "l_x", 8000)
    dma(r("nzs", 0, A), T.nz[:], "l_nz", 8200)
    dma(r("nzs", A, A + 8), T.nz[:, 0:8], "l_nw", 8200)

    place[0] = (-9.0, 0)
    fill(r("one"), 1.0)
    fill(r("exa", 0, 768, 1, 32), 3 * BIG)
    fill(r("exc", 0, 512, 1, 32), -1.0)
    fill(r("ph"), 8.0)
    fill(r("rst"), 0.0)
    fill(r("rs2"), 0.0)
    for c, x in enumerate((MAG, -MAG)):
        fill(half("mg", c, 8), x)
    fill(r("rst", 0, 128, 16), -2.0 ** 26)
    fill(r("rs2", 0, 256, 32), 2.0 ** 30)
    fill(r("rs2", 256, 768, 64), 2.0 ** 30)
    scan(r("num"), r("ph"), r("ph"), -16.0, OP.add, OP.add)
    iota(r("ia", 128, 144), [[1, 16]], 1, 1)
    iota(r("ia", 0, 128), [[1, 128]], 128, -1)
    iota(r("ia", 144, 152), [[16, 8]], 15, 0)
    iota(r("ia", 152, 160), [[0, 4], [16, 2]], V, 0)
    iota(r("ia", 160, 176), [[0, 4], [16, 4]], V, 0)
    select(r("idb"), r("one", 0, 128), [[-1, 128]], OP.is_equal, 0.0, 0, 1)
    select(r("bo", 128, 256), r("one", 0, 128), [[-16, 8], [0, 16]], OP.is_ge, 0.0, 0, 1)
    a, b = r("exa", 0, 256, 1, 32), r("exb", 0, 256, 1, 32)
    select(b, a, [[-16, 2], [0, 4], [1, 32]], OP.is_gt, BIG, 16, -1)
    select(r("bo", 0, 128), r("bo", 128, 256), [[16, 8], [0, 16]], OP.is_ge, 0.0, 15, -1)
    post(nxt, r("z1"), r("z0"), "a_z1")
    post(two, r("z2"), r("z0"), "a_z2")
    select(a, b, [[-16, 2], [0, 4], [1, 32]], OP.not_equal, 0.0, 16, -1)
    select(r("exa", 0, 256, 1, 16), r("exc", 0, 256, 1, 16), [[1, 2], [2, 4], [0, 32]], OP.is_equal, 0.0, 0, -1)
    group = r("bo", 0, 128, 16)
    ts(r("ib"), r("ia", 0, 144), 15, OP.bitwise_and)
    for h in (1, 0):
        copy(half("vl", 4 * h, 8), half("v0s", h, 8))
    row = col(0)
    copy(row, r("ib", 143, 144))
    ts(col(2), r("ib", 143, 144), -1.0, OP.mult, 15.0, OP.add)
    ts(r("spare"), r("ia", 152, 176), row, OP.add)
    ts(r("msk"), r("ib", 0, 128), 0.0, OP.is_equal)
    ts(r("wk", 0, 16), r("ib", 128, 144), 0.0, OP.is_equal, 11.0, OP.mult)
    for k in range(16):
        if k % 2:
            copy(r("zr0", k, 16 * A, 16), r("z0"))
        else:
            act(r("zr0", k, 16 * A, 16), r("z0"), AF.Copy)
    copy(r("bc"), r("ia", 144, 152))
    for name, c in (("idh", 1.0), ("idk", 2048.0), ("idp", 32768.0), ("idm", -BIG), ("idn", -1.0)):
        ts(r(name), r("idb"), c, OP.mult)
    ts(r("gw", 0, 8), group, -65536.0, OP.mult)
    ts(r("gw", 8, 16), group, 32768.0, OP.mult)
    for c, x in enumerate((-1.0, 2.0)):
        ts(half("bw", c), half("bo", 0), x, OP.mult)
    copy(r("g2", 0, 8), group)
    ts(r("g2", 8, 16), group, -1.0, OP.mult)
    ts(r("dtab", 0, 16), r("wk", 0, 16), -3.0, OP.add)
    ts(r("dtab", 16, 32), r("wk", 0, 16), 5.0, OP.add)
    for e in range(2 * ST):
        act(r("ut", 128 * e, 128 * e + 128, 1, 32), r("msk", 0, 128, 1, 32), AF.Copy)
    place[0] = (6.5, 5)
    act(r("exh", 0, 256, 1, 32), a, AF.Copy)
    place[0] = None
    ts(r("nzk"), r("nzs"), 16.0, OP.mult, col(2), OP.add)

    def spread(i, k):
        select(r(zr[i], k, 16 * A, 16), r(zz[i]), [[0, A]], OP.is_ge, 0.0, 0, 0)

    def wide_exh(e):
        a, b = r("exa", 256, 768, 1, 32), r("exb", 256, 768, 1, 32)
        if e < 2:
            select(*((a, b) if e else (b, a)), [[0, 2], [-16, 4], [1, 64]], OP.not_equal if e else OP.is_gt, 0.0 if e else BIG, 16, -1)
        else:
            select(r("exa", 256, 768, 1, 16), r("exc", 0, 512, 1, 16), [[1, 8], [0, 64]], OP.is_equal, 0.0, 0, -1)
            act(r("exh", 256, 768, 1, 32), a, AF.Copy)

    later = [(wide_exh, e) for e in range(3)] + [(lambda k: spread(2, k), k) for k in range(16)]

    def ish(j):
        return j // 6, (j % 6) // 2, 1 - j % 2

    def nodes(slot, h):
        return half("vl", 8 * (slot // 4) + 4 * h + slot % 4, 8)

    def cuts(a, b, most):
        m = -(-(b - a) // most)
        e = [a + 2 * (((b - a) // 2 * t) // max(m, 1)) for t in range(m + 1)]
        return [(e[t], e[t + 1]) for t in range(m)]

    bank = [0]

    def half_step(j):
        i, s, h = ish(j)
        kb, a = "kb%d" % h, 128 * h + 3 * i + s
        keys = r(kb, 0, 128)
        wide = lambda name, a, b: r(name, 16 * (128 * h + a), 16 * (128 * h + b))
        feats = lambda a, b: ind(r("xs"), r("nm", 128 * h + a, 128 * h + b))
        at(j, "names", copy, half("nm", h), ind(r("adjs"), nodes(4 * i + s, h)))
        at(j, "centred", ts, half("ee", h), half("nm", h), float(-OFF), OP.add)
        at(j, "open", mm, keys, r("nzk", a, a + 128), r("idk"), True)
        cut = CUT[KIND[j]]
        na, nc = cut[0] + cut[1], sum(cut[:3])
        for t, (a, b) in enumerate([(nc, nc + min(AC, cut[3]))] + cuts(nc + min(AC, cut[3]), 128, AC)):
            sb = r("sb%d" % (bank[0] % 3), 0, 16 * (b - a))
            bank[0] += 1
            at(j, "g%d" % t, act, wide("dd", a, b), feats(a, b), AF.Copy)
            at(j, "z%d" % t, mm, sb, r("idn"), wide(zr[i], a, b), True)
            at(j, "x%d" % t, mm, sb, r("idb"), wide("dd", a, b), False)
            at(j, "a%d" % t, act, wide("rr", a, b), sb, AF.Abs, 0.5)
        for t in range(3):
            a, b = sum(cut[:t]), sum(cut[:t + 1])
            if b > a:
                at(j, "v%d" % t, tt, wide("dd", a, b), feats(a, b), wide(zr[i], a, b), OP.subtract)
                if t < 2:
                    at(j, "relu%d" % t, ts, wide("rr", a, b), wide("dd", a, b), 0.0, OP.max)
                else:
                    at(j, "abs", act, wide("rr", a, b), wide("dd", a, b), AF.Abs, 0.5)
        for k in range(16 if na else 0):
            at(j, "sumd", mm, r(kb, k, 128, 16, na), r("dd", 2048 * h + k, 2048 * h + 16 * na, 16), r("gw", 8, 16), False)
        at(j, "name", mm, keys, half("ee", h), r("idh"), False)
        if j >= 14:
            at(j, "ph0", act, half("phg", h), ind(r("ph"), nodes(4 * i + s, h)), AF.Copy)
            at(j, "name", mm, keys, half("phg", h), r("idp"), False)
        for k in range(16):
            at(j, "sum", mm, r(kb, k, 128, 16), r("rr", 2048 * h + k, 2048 * h + 2048, 16), r("gw", 0, 8), False)

    def choice(j):
        i, s, h = ish(j)
        kb = "kb%d" % h
        keys = r(kb, 0, 128)
        if j in (12, 13):
            at(j, "ph", act, half("phg", h), ind(r("ph"), nodes(4 * i + s, h)), AF.Copy)
            at(j, "close", mm, keys, half("phg", h), r("idp"), False)
        at(j, "best", scan, half("sc", h), r("rst"), keys, 0.0, OP.add, OP.max)
        at(j, "widen", tt, half("ll", h), ind(half("sc", h), r("bc")), r("msk"), OP.mult)
        right = r(kb, 408 + s, 432, 3)
        at(j, "turn", mm, r(kb, 384 + s, 432, 3), half("ll", h), r("g2"), True)
        at(j, "turn", mm, right, r("idb"), r("mg", 0, 8), False)
        at(j, "turn", mm, right, r("idb"), r("mg", 8, 16), False)
        at(j, "turn", mm, right, half("ll", h), r("g2", 0, 8), False)
        if s == ST - 1 and "chosenv" in [k for k, d in ORDER["V"]]:
            at(j, "chosenv", ts, nodes(4 * i + s + 1, h), right, float(OFF), OP.add)
        else:
            at(j, "chosen", act, nodes(4 * i + s + 1, h), right, AF.Identity, 1.0, float(OFF))
        if s == ST - 1:
            if i < VIS - 1:
                post(nxt, nodes(4 * i + 4, h), nodes(4 * i + 3, h), "a_v%d%d" % (i + 1, h))
                ts(half("ki", h, 24), r(kb, 384, 408), float(OFF), OP.add)
            distance(j)

    def distance(j):
        i, s, h = ish(j)
        far = r("kb%d" % h, 256, 384)
        at(j, "end", tt, half("fd", h), ind(r("xs"), nodes(4 * i + 3, h)), half(zz[i], h), OP.subtract)
        at(j, "endabs", ts, half("fa", h), half("fd", h), 0.0, OP.max)
        at(j, "far", mm, far, half("bw", 0), half("fd", h), True)
        at(j, "far", mm, far, half("bw", 1), half("fa", h), False)
        if i > 0:
            at(j, "flag", tt, half("fo%d" % i, h), far, half("di%d" % (i - 1), h), OP.is_lt)
            post(prv, half("fi%d" % i, h), half("fo%d" % i, h), "a_f%d%d" % (i, h))
        if i < VIS - 1:
            act(half("do%d" % i, h), far, AF.Copy)

    def trail(i, h):
        def part(name, slots):
            return lambda a=0, b=None: r(name, 8 * (slots * h + a), 8 * (slots * h + (a + 1 if b is None else b)))
        vf, nn, w = part("vf", 4), part("nn", 5), part("wk", 11)
        pp, ex, kb, un, kr, y0, ku, uh, yy, ul = [part(x, 3) for x in ("pp", "ex", "kb", "un", "kr", "y0", "ku", "uh", "yy%d" % i, "ul%d" % i)]
        copy(vf(0, 4), r("vl", 64 * i + 32 * h, 64 * i + 32 * h + 32))
        ts(kb(0, 3), half("ki", h, 24), 15 << 11, OP.bitwise_and)
        tt(nn(0, 3), vf(0, 3), vf(1, 4), OP.not_equal)
        tt(nn(3, 5), vf(0, 2), vf(2, 4), OP.not_equal)
        tt(ex(0), vf(0), vf(3), OP.not_equal)
        for s in range(ST):
            tt(pp(s), r("kb", 24 * h + s, 24 * h + 24, 3), vf(s), OP.add)
        tt(w(2), nn(0), nn(3), OP.mult)
        tt(w(3), nn(0), nn(1), OP.mult)
        tt(w(7), nn(3), nn(4), OP.mult)
        tt(w(0, 2), pp(1, 3), pp(0, 2), OP.subtract)
        tt(w(9), nn(0), nn(2), OP.max)
        tt(w(10), w(3), nn(2), OP.mult)
        tt(w(8), w(7), ex(0), OP.mult)
        tt(w(4, 6), w(2, 4), w(0, 2), OP.mult)
        tt(w(6), nn(3), w(1), OP.mult)
        tt(ex(1, 3), r("wk", 88 * h + 72, 88 * h + 88), r("wk", 88 * h + 64, 88 * h + 80), OP.min)
        tt(ex(2), ex(1), ex(2), OP.min)
        tt(pp(1), pp(2), w(5), OP.subtract)
        tt(w(7), w(4), w(6), OP.add)
        tt(pp(0), pp(2), w(7), OP.subtract)
        ts(un(0, 3), pp(0, 3), 2047, OP.bitwise_and)
        ts(kr(0, 3), pp(0, 3), 11, OP.arith_shift_right)
        tt(y0(0, 3), r("spare"), un(0, 3), OP.subtract)
        copy(ku(0, 3), kr(0, 3))
        tt(yy(0, 3), y0(0, 3), ex(0, 3), OP.mult)
        tt(uh(0, 3), r("spare"), yy(0, 3), OP.subtract)
        copy(ul(0, 3), uh(0, 3))
        if i == 0:
            act(half("tc", h), ind(r("dtab", 16, 32), ku(0)), AF.Copy)
        act(r("dl%d" % i, 384 * h + 128 * (1 - i), 384 * h + 384), ind(r("dtab", 0, 16), ku(1 - i, 3)), AF.Copy)

    def turned(i, h):
        sb = "sb%d" % (bank[0] % 3)
        bank[0] += 1
        for p in range(ST):
            mm(r(sb, 128 * p, 128 * p + 128, 1, 8), half("uh", 3 * h + p, 8), r("idh"), True)
        act(r("ut", 384 * h, 384 * h + 384, 1, 8), r(sb, 0, 384, 1, 8), AF.Copy)
        act(half("um", h, 384), ind(r("num"), half("ul%d" % i, h, 24)), AF.Copy, 1.0 / 16)

    def spread_over(p, lhsT, name, c):
        if p == 0:
            for t in (0, 1):
                mm(half("px0", t), lhsT, r(name, c, c + 128), False)
        else:
            for e in range(8):
                mm(half("px%d" % p, e, 64), lhsT, r(name, c + 64 * (e // 4), c + 64 * (e // 4) + 64), False)

    def differences(h):
        for p in range(ST):
            c, (a, m) = 384 * h + 128 * p, ((256, 512) if p else (0, 256))
            mm(r("px%d" % p, 0, m), r("ut", c, c + 128, 1, 32), r("exh", a, a + m, 1, 32), True)
            spread_over(p, r("idh"), "um", c)

    def winners(i, h):
        for p in range(ST):
            c, m = 1280 * h + 512 * p - 256 * (p > 0), 512 if p else 256
            spread_over(p, r("idm"), "fi%d" % (i + 1), 128 * h)
            act(r("ab", c, c + m), r("px%d" % p, 0, m), AF.Abs, BIG)
            scan(r("pr", c, c + m), r("rs2", 256 * (p > 0), 256 * (p > 0) + m), r("ab", c, c + m), 0.0, OP.add, OP.min)
        for t in (0, 1):
            mine = lambda name: r(name, 24 * h + t, 24 * h + 8, 2)
            tt(mine("ok"), r("pr", 1280 * h + 128 * t + 31, 1280 * h + 128 * t + 128, 32), mine("yy%d" % i), OP.min)
            ts(mine("lst"), mine("ok"), -1.0, OP.mult, r("spare", t, t + 1), OP.add)
        for p0, p1 in ((1, 3),) if h else ((1, 2), (2, 3)):
            mine = lambda name: r(name, 24 * h + 8 * p0, 24 * h + 8 * p1)
            tt(mine("ok"), r("pr", 1280 * h + 512 * p0 - 256 + 63, 1280 * h + 512 * p1 - 256, 64), mine("yy%d" % i), OP.min)
            tt(mine("lf"), r("spare", 8 * p0, 8 * p1), mine("ok"), OP.subtract)
            copy(mine("lst"), mine("lf"))

    def renewed(i, p, halves=(1, 0)):
        for h in halves:
            tt(half("tm", h), ind(r("ph"), half("ul%d" % i, 3 * h + p, 8)), half("dl%d" % i, 3 * h + p), OP.add)
        for h in halves:
            ts(half("tc", h), half("tm", h), 0.0, OP.max, 20.0, OP.min)

    def reinforce(i):
        winners(i, 1)
        differences(0)
        winners(i, 0)
        for p in range(ST):
            if p > 0:
                renewed(i, p)
            m = 4 if p else 2
            for c in range(16 - m, -1, -m):
                e = 24 * (c // 8) + 8 * p + c % 8
                copy(ind(r("ph"), r("lst", e, e + m)), r("tc", 16 * c, 16 * (c + m)))

    for k in range(16):
        spread(1, k)
    for fn, e in later[:NUM["early"]]:
        fn(e)
    for i in range(VIS):
        for j in range(6 * i, 6 * i + 6):
            half_step(j)
            if j == 13:
                reinforce(0)
                renewed(1, 0)
                choice(12)
            if j != 12:
                choice(j)
            for e in (0, 1):
                for h in (1, 0):
                    if j == NUM["turn%d%d" % (e, h)]:
                        turned(e, h)
                        if h:
                            differences(1)
            if j in (4, 5, 10, 11):
                trail(i, 1 - j % 2)
        if i < VIS - 1:
            post(nxt, r("di%d" % i), r("do%d" % i), "a_d%d" % i)
        if i == 0:
            for fn, e in later[NUM["early"]:]:
                fn(e)
    for h in (1, 0):
        copy(half("yvs", h, 8), nodes(11, h))
    dma(T.yv[:], r("yvs"), "s_yv", 2500)
    reinforce(1)
    dma(T.yp[:], r("ph", 0, V), "s_yp", 4000)

    if not PLAN:
        hard, soft = links(ops)
        PLAN.extend([hard, arrange(ops, hard, soft)])
    hard, order = PLAN
    waits, total = plan_waits(ops, hard, order)
    for o in order:
        q, sem, inc, emit = ops[o][0], ops[o][1], ops[o][2], ops[o][5]
        if emit is None:
            continue
        for s, c in waits[o]:
            Q[q].wait_ge(T.sem[s], c)
        ins = emit()
        if sem is not None:
            ins.then_inc(T.sem[sem], inc)
    g.wait_ge(T.sem.sent, width * len(posts))
    for s in ENG + ("s_yv", "s_yp"):
        g.sync.wait_ge(T.sem[s], total[s])
